import numpy as np
import ml_dtypes


def mxq(x, axis, fmt="e4m3"):
    dtype, down = {"e4m3": (ml_dtypes.float8_e4m3fn, 7), "e5m2": (ml_dtypes.float8_e5m2, 14)}[fmt]
    v = np.moveaxis(np.asarray(x, np.float32).astype(ml_dtypes.bfloat16).astype(np.float64), axis, -1)
    blocks = v.reshape(v.shape[:-1] + (-1, 32))
    amax = np.abs(blocks).max(-1, keepdims=True)
    byte = np.maximum(np.where(amax > 0, np.frexp(amax)[1] - 1 + 127, 0) - down, 1)
    scale = np.exp2(byte - 127.0)
    codes = (blocks / scale).astype(np.float32).astype(dtype).astype(np.float64)
    return np.moveaxis((codes * scale).reshape(v.shape), -1, axis)


WIDE = False


def mx_kscale(k):
    if not WIDE:
        return np.ones(k)
    levels = np.array([10, -10, 5, -5, 0])
    if k % 512:
        return np.exp2(np.random.permutation(np.resize(levels, k // 32))).repeat(32)
    a = np.empty((k // 512, 16))
    for p in range(k // 512):
        a[p, :8] = np.random.permutation(np.resize(levels, 8))
        for g in range(8):
            far = levels[np.abs(levels - a[p, g]) >= 10]
            a[p, g + 8] = far[np.random.randint(len(far))]
    return np.exp2(a.ravel()).repeat(32)


def f64(x):
    return np.asarray(x).astype(np.float64)


def striped(idx):
    return np.tile(idx.reshape(-1, 16).T, (8, 1)).astype(np.uint16)


def unstriped(offs):
    return offs[:16].T.reshape(-1).astype(np.int64)


def pack_weight(w):
    k, n = w.shape
    w = f64(np.asarray(w, np.float32).astype(ml_dtypes.bfloat16)).reshape(k // 32, 32, n)
    amax = np.abs(w).max(1)
    byte = np.clip(np.where(amax > 0, np.frexp(amax)[1] - 1 + 127 - 7, 1), 1, 254)
    scaled = (w * np.exp2(127.0 - byte)[:, None, :]).reshape(k, n).astype(np.float32)
    words = np.ascontiguousarray(scaled.reshape(k // 512, 128, 4, n).transpose(0, 1, 3, 2)).astype(ml_dtypes.float8_e4m3fn).view(np.uint8)
    return words, np.ascontiguousarray(byte.astype(np.uint8).reshape(k // 512, 16, n))


def unpack_weight(words, scales):
    g, p, n, _ = words.shape
    vals = np.ascontiguousarray(words).view(ml_dtypes.float8_e4m3fn).astype(np.float64) * np.repeat(np.exp2(scales.astype(np.float64) - 127.0), 8, axis=1)[..., None]
    return vals.transpose(0, 1, 3, 2).reshape(g * 512, n)


def sigmoid(v):
    return 1.0 / (1.0 + np.exp(-np.maximum(v, -700.0)))


K, T, S, N = 1024, 2048, 512, 256


def setup_inputs():
    n = np.random.standard_normal
    s = mx_kscale(K)[:, None]
    packed_xT = pack_weight(n((K, T)) * s)
    return {
        "x_words": packed_xT[0],
        "x_scales": packed_xT[1],
        "w1": (n((K, N)) / np.sqrt(K) / s).astype(np.float32),
        "w2": (n((K, N)) / np.sqrt(K) / s).astype(np.float32),
        "w3": (n((K, N)) / np.sqrt(K) / s).astype(np.float32),
        "cell": n((N, T)).astype(np.float32),
        "offs": striped(np.random.permutation(T)[(T * np.random.uniform(0, 1, S) ** 4).astype(np.int64)]),
    }


def reference(x_words, x_scales, w1, w2, w3, cell, offs):
    xq = unpack_weight(x_words, x_scales)[:, unstriped(offs)]
    f = sigmoid(mxq(f64(w1), 0, "e4m3").T @ xq)
    r = f64(cell)[:, unstriped(offs)]
    i = sigmoid(mxq(f64(w2), 0, "e4m3").T @ xq)
    g = np.tanh(mxq(f64(w3), 0, "e4m3").T @ xq)
    return f * r + i * g

@@ -1,0 +1,135 @@
+from contextlib import ExitStack
+
+import concourse.mybir as mybir
+
+K, T, S, N = 1024, 2048, 512, 256
+FLOPS = 3 * 2 * K * N * S
+
+F32 = mybir.dt.float32
+BF16 = mybir.dt.bfloat16
+I32 = mybir.dt.int32
+U32 = mybir.dt.uint32
+U16 = mybir.dt.uint16
+U8 = mybir.dt.uint8
+FP8X4 = mybir.dt.float8_e4m3fn_x4
+ACT = mybir.ActivationFunctionType
+ALU = mybir.AluOpType
+
+P = 128
+PACK = 4
+K_PASS = P * PACK
+PASSES = K // K_PASS
+BLOCKS = N // P
+
+
+def tile_picked_beamcell_none_p_kernel(tc, x_words, x_scales, w1, w2, w3, cell, offs, out):
+    nc = tc.nc
+    with ExitStack() as ctx:
+        sb = ctx.enter_context(tc.tile_pool(name="sb", bufs=1))
+        ps = ctx.enter_context(tc.psum_pool(name="ps", bufs=1))
+
+        def load_w(w, gate, z):
+            raw = sb.tile([P, PACK, N], F32, name=f"raw_{gate}{z}")
+            nc.sync.dma_start(out=raw[:], in_=w[z * K_PASS:(z + 1) * K_PASS, :].rearrange("(p j) n -> p j n", j=PACK))
+            return raw
+
+        def load_x(z):
+            table = sb.tile([P, T], U32, name=f"words{z}")
+            nc.sync.dma_start(out=table[:].bitcast(I32), in_=x_words[z].rearrange("p n t -> p (n t)").bitcast(I32))
+            return table
+
+        def load_cell(b):
+            rows = sb.tile([P, T], F32, name=f"cell{b}")
+            nc.sync.dma_start(out=rows[:], in_=cell[b * P:(b + 1) * P, :])
+            return rows
+
+        def interleave(copy, raw, c0, c1, name):
+            grouped = sb.tile([P, c1 - c0, PACK], BF16, name=name, align_bytes=64)
+            copy(out=grouped[:].rearrange("p (c i) t -> p c t i", i=4),
+                 in_=raw[:, :, c0:c1].rearrange("p t (c i) -> p c t i", i=4))
+            return grouped
+
+        def quantize(grouped, width, name):
+            codes = sb.tile([P, width], U32, name=f"codes_{name}", align_bytes=64)
+            scales = sb.tile([P, width], U8, name=f"scales_{name}", align_bytes=64)
+            nc.vector.quantize_mx(out=codes[:].bitcast(FP8X4), scales=scales[:],
+                                  in_=grouped[:].rearrange("p c t -> p (c t)"))
+            return codes, scales
+
+        scale_table = sb.tile([P, T], U8, name="scale_table")
+        nc.vector.memset(scale_table[:].bitcast(I32), 0)
+
+        raw = {}
+        raw["i", 0] = load_w(w2, "i", 0)
+        offsets = sb.tile([P, S // 16], U16, name="offsets")
+        nc.sync.dma_start(offsets[:], offs)
+        for q in range(4):
+            nc.scalar.dma_start(out=scale_table[32 * q:32 * q + 4 * PASSES, :].bitcast(I32),
+                                in_=x_scales[:, 4 * q:4 * q + 4, :].bitcast(I32))
+        raw["i", 1] = load_w(w2, "i", 1)
+        tables = [load_x(0)]
+        raw["g", 0] = load_w(w3, "g", 0)
+        tables.append(load_x(1))
+        raw["g", 1] = load_w(w3, "g", 1)
+        for z in range(PASSES):
+            raw["f", z] = load_w(w1, "f", z)
+        cells = [load_cell(b) for b in range(BLOCKS)]
+
+        x_sc = sb.tile([P, S], U8, name="x_sc", align_bytes=64)
+        nc.vector.tensor_copy(x_sc[:], scale_table[:].indirect(offsets[:]))
+
+        acc = {(gate, b): ps.tile([P, S], F32, name=f"acc_{gate}{b}") for gate in "gif" for b in range(BLOCKS)}
+        x_codes = {}
+
+        def gather_x(z):
+            x_codes[z] = sb.tile([P, S], U32, name=f"x_codes{z}", align_bytes=64)
+            nc.vector.tensor_copy(x_codes[z][:], tables[z][:].indirect(offsets[:]))
+
+        def multiply(gate, b, z, codes, scales):
+            nc.tensor.matmul_mx(out=acc[gate, b][:], lhsT=codes.bitcast(FP8X4), lhsT_scale=scales,
+                                rhs=x_codes[z][:].bitcast(FP8X4), rhs_scale=x_sc[4 * z:P, :],
+                                start=(z == 0), stop=(z == PASSES - 1))
+
+        def whole(gate, z, copy):
+            return quantize(interleave(copy, raw[gate, z], 0, N, f"bf_{gate}{z}"), N, f"{gate}{z}")
+
+        def both(gate, z, pair):
+            for b in range(BLOCKS):
+                multiply(gate, b, z, pair[0][:, b * P:(b + 1) * P], pair[1][:, b * P:(b + 1) * P])
+
+        act = {}
+
+        def activate(gate, b, func):
+            act[gate, b] = sb.tile([P, S], F32, name=f"act_{gate}{b}")
+            nc.scalar.activation(out=act[gate, b][:], in_=acc[gate, b][:], func=func)
+
+        vcopy = nc.vector.tensor_copy
+        wi = [whole("i", z, vcopy) for z in range(PASSES)]
+        gather_x(0)
+        both("i", 0, wi[0])
+        both("g", 0, whole("g", 0, vcopy))
+        gather_x(1)
+        both("i", 1, wi[1])
+        for b in range(BLOCKS):
+            activate("i", b, ACT.Sigmoid)
+        both("g", 1, whole("g", 1, vcopy))
+        for b in range(BLOCKS):
+            activate("g", b, ACT.Tanh)
+        both("f", 0, whole("f", 0, vcopy))
+        new = {}
+        for b, copy in enumerate((vcopy, nc.scalar.copy)):
+            codes, scales = quantize(interleave(copy, raw["f", 1], b * P, (b + 1) * P, f"bf_f1{b}"), P, f"f1{b}")
+            multiply("f", b, 1, codes[:], scales[:])
+            activate("f", b, ACT.Sigmoid)
+            new[b] = sb.tile([P, S], F32, name=f"new{b}")
+            nc.vector.tensor_tensor(new[b][:], act["i", b][:], act["g", b][:], ALU.mult)
+        H = S // 2
+        for b in range(BLOCKS):
+            kept = [sb.tile([P, H], F32, name=f"kept{b}{h}") for h in range(2)]
+            for h in range(2):
+                nc.vector.tensor_tensor(kept[h][:], cells[b][:].indirect(offsets[:, h * H // 16:(h + 1) * H // 16]),
+                                        act["f", b][:, h * H:(h + 1) * H], ALU.mult)
+            for h in range(2):
+                res = sb.tile([P, H], F32, name=f"res{b}{h}")
+                nc.vector.tensor_tensor(res[:], kept[h][:], new[b][:, h * H:(h + 1) * H], ALU.add)
+                nc.sync.dma_start(out=out[b * P:(b + 1) * P, h * H:(h + 1) * H], in_=res[:])

@@ -34,12 +34,12 @@ def tile_picked_beamcell_none_p_kernel(tc, x_words, x_scales, w1, w2, w3, cell, 
             return raw
 
         def load_x(z):
-            table = sb.tile([P, T], U32, name=f"words{z}")
+            table = sb.tile([P, T], U32, name=f"words{z}", tag=f"table{z}")
             nc.sync.dma_start(out=table[:].bitcast(I32), in_=x_words[z].rearrange("p n t -> p (n t)").bitcast(I32))
             return table
 
         def load_cell(b):
-            rows = sb.tile([P, T], F32, name=f"cell{b}")
+            rows = sb.tile([P, T], F32, name=f"cell{b}", tag=f"table{b}")
             nc.sync.dma_start(out=rows[:], in_=cell[b * P:(b + 1) * P, :])
             return rows
 
@@ -56,27 +56,28 @@ def tile_picked_beamcell_none_p_kernel(tc, x_words, x_scales, w1, w2, w3, cell, 
                                   in_=grouped[:].rearrange("p c t -> p (c t)"))
             return codes, scales
 
-        scale_table = sb.tile([P, T], U8, name="scale_table")
-        nc.vector.memset(scale_table[:].bitcast(I32), 0)
+        scale_table = sb.tile([P, PASSES * T], U8, name="scale_table")
+        nc.vector.memset(scale_table[:, :2304].bitcast(I32), 0)
+        nc.gpsimd.memset(scale_table[:, 2304:].bitcast(I32), 0)
+        warm = sb.tile([P, 2], F32, name="warm")
+        nc.vector.memset(warm[:, 0:1], 0.0)
+        nc.scalar.activation(out=warm[:, 1:2], in_=warm[:, 0:1], func=ACT.Sigmoid)
+        x_sc = sb.tile([P, PASSES * S], U8, name="x_sc", align_bytes=64)
+        nc.gpsimd.memset(x_sc[:].bitcast(I32), 0)
 
         raw = {}
         raw["i", 0] = load_w(w2, "i", 0)
         offsets = sb.tile([P, S // 16], U16, name="offsets")
         nc.sync.dma_start(offsets[:], offs)
-        for q in range(4):
-            nc.scalar.dma_start(out=scale_table[32 * q:32 * q + 4 * PASSES, :].bitcast(I32),
-                                in_=x_scales[:, 4 * q:4 * q + 4, :].bitcast(I32))
         raw["i", 1] = load_w(w2, "i", 1)
+        nc.sync.dma_start(out=scale_table[4:P:8, :].bitcast(I32).rearrange("r (z c) -> r z c", z=PASSES),
+                          in_=x_scales.bitcast(I32).rearrange("z r c -> r z c"))
         tables = [load_x(0)]
         raw["g", 0] = load_w(w3, "g", 0)
         tables.append(load_x(1))
         raw["g", 1] = load_w(w3, "g", 1)
         for z in range(PASSES):
             raw["f", z] = load_w(w1, "f", z)
-        cells = [load_cell(b) for b in range(BLOCKS)]
-
-        x_sc = sb.tile([P, S], U8, name="x_sc", align_bytes=64)
-        nc.vector.tensor_copy(x_sc[:], scale_table[:].indirect(offsets[:]))
 
         acc = {(gate, b): ps.tile([P, S], F32, name=f"acc_{gate}{b}") for gate in "gif" for b in range(BLOCKS)}
         x_codes = {}
@@ -87,7 +88,7 @@ def tile_picked_beamcell_none_p_kernel(tc, x_words, x_scales, w1, w2, w3, cell, 
 
         def multiply(gate, b, z, codes, scales):
             nc.tensor.matmul_mx(out=acc[gate, b][:], lhsT=codes.bitcast(FP8X4), lhsT_scale=scales,
-                                rhs=x_codes[z][:].bitcast(FP8X4), rhs_scale=x_sc[4 * z:P, :],
+                                rhs=x_codes[z][:].bitcast(FP8X4), rhs_scale=x_sc[:, z * S:(z + 1) * S],
                                 start=(z == 0), stop=(z == PASSES - 1))
 
         def whole(gate, z, copy):
@@ -104,32 +105,41 @@ def tile_picked_beamcell_none_p_kernel(tc, x_words, x_scales, w1, w2, w3, cell, 
             nc.scalar.activation(out=act[gate, b][:], in_=acc[gate, b][:], func=func)
 
         vcopy = nc.vector.tensor_copy
-        wi = [whole("i", z, vcopy) for z in range(PASSES)]
+        picked_sc = sb.tile([P, PASSES * S], U8, name="picked_sc")
+        for z in range(PASSES):
+            nc.vector.tensor_copy(picked_sc[:, z * S:(z + 1) * S], scale_table[:, z * T:(z + 1) * T].indirect(offsets[:]))
+        for q in range(4):
+            nc.scalar.dma_start(out=x_sc[32 * q:32 * q + 4, :].bitcast(I32),
+                                in_=picked_sc[32 * q + 4:32 * q + 32:8, :].bitcast(I32))
+        wi = [whole("i", z, nc.scalar.copy) for z in range(PASSES)]
         gather_x(0)
-        both("i", 0, wi[0])
-        both("g", 0, whole("g", 0, vcopy))
+        wg = [whole("g", 0, nc.scalar.copy)]
         gather_x(1)
-        both("i", 1, wi[1])
+        for z in range(PASSES):
+            both("i", z, wi[z])
         for b in range(BLOCKS):
             activate("i", b, ACT.Sigmoid)
-        both("g", 1, whole("g", 1, vcopy))
+        wg.append(whole("g", 1, vcopy))
+        for z in range(PASSES):
+            both("g", z, wg[z])
         for b in range(BLOCKS):
             activate("g", b, ACT.Tanh)
         both("f", 0, whole("f", 0, vcopy))
         new = {}
-        for b, copy in enumerate((vcopy, nc.scalar.copy)):
+        for b, copy in enumerate((vcopy, vcopy)):
             codes, scales = quantize(interleave(copy, raw["f", 1], b * P, (b + 1) * P, f"bf_f1{b}"), P, f"f1{b}")
             multiply("f", b, 1, codes[:], scales[:])
             activate("f", b, ACT.Sigmoid)
             new[b] = sb.tile([P, S], F32, name=f"new{b}")
             nc.vector.tensor_tensor(new[b][:], act["i", b][:], act["g", b][:], ALU.mult)
-        H = S // 2
-        for b in range(BLOCKS):
-            kept = [sb.tile([P, H], F32, name=f"kept{b}{h}") for h in range(2)]
-            for h in range(2):
+        cells = [load_cell(b) for b in range(BLOCKS)]
+        for b, pieces in enumerate((1, 2)):
+            H = S // pieces
+            kept = [sb.tile([P, H], F32, name=f"kept{b}{h}") for h in range(pieces)]
+            for h in range(pieces):
                 nc.vector.tensor_tensor(kept[h][:], cells[b][:].indirect(offsets[:, h * H // 16:(h + 1) * H // 16]),
                                         act["f", b][:, h * H:(h + 1) * H], ALU.mult)
-            for h in range(2):
+            for h in range(pieces):
                 res = sb.tile([P, H], F32, name=f"res{b}{h}")
                 nc.vector.tensor_tensor(res[:], kept[h][:], new[b][:, h * H:(h + 1) * H], ALU.add)
                 nc.sync.dma_start(out=out[b * P:(b + 1) * P, h * H:(h + 1) * H], in_=res[:])

@@ -28,8 +28,8 @@ def tile_picked_beamcell_none_p_kernel(tc, x_words, x_scales, w1, w2, w3, cell, 
         sb = ctx.enter_context(tc.tile_pool(name="sb", bufs=1))
         ps = ctx.enter_context(tc.psum_pool(name="ps", bufs=1))
 
-        def load_w(w, gate, z):
-            raw = sb.tile([P, PACK, N], F32, name=f"raw_{gate}{z}")
+        def load_w(w, gate, z, tag):
+            raw = sb.tile([P, PACK, N], F32, name=f"raw_{gate}{z}", tag=tag)
             nc.sync.dma_start(out=raw[:], in_=w[z * K_PASS:(z + 1) * K_PASS, :].rearrange("(p j) n -> p j n", j=PACK))
             return raw
 
@@ -38,13 +38,13 @@ def tile_picked_beamcell_none_p_kernel(tc, x_words, x_scales, w1, w2, w3, cell, 
             nc.sync.dma_start(out=table[:].bitcast(I32), in_=x_words[z].rearrange("p n t -> p (n t)").bitcast(I32))
             return table
 
-        def load_cell(b):
-            rows = sb.tile([P, T], F32, name=f"cell{b}", tag=f"table{b}")
+        def load_cell(b, tag):
+            rows = sb.tile([P, T], F32, name=f"cell{b}", tag=tag)
             nc.sync.dma_start(out=rows[:], in_=cell[b * P:(b + 1) * P, :])
             return rows
 
         def interleave(copy, raw, c0, c1, name):
-            grouped = sb.tile([P, c1 - c0, PACK], BF16, name=name, align_bytes=64)
+            grouped = sb.tile([P, c1 - c0, PACK], BF16, name=name, tag=name, align_bytes=64)
             copy(out=grouped[:].rearrange("p (c i) t -> p c t i", i=4),
                  in_=raw[:, :, c0:c1].rearrange("p t (c i) -> p c t i", i=4))
             return grouped
@@ -56,7 +56,7 @@ def tile_picked_beamcell_none_p_kernel(tc, x_words, x_scales, w1, w2, w3, cell, 
                                   in_=grouped[:].rearrange("p c t -> p (c t)"))
             return codes, scales
 
-        scale_table = sb.tile([P, PASSES * T], U8, name="scale_table")
+        scale_table = sb.tile([P, PASSES * T], U8, name="scale_table", tag="scale_table")
         nc.vector.memset(scale_table[:, :2304].bitcast(I32), 0)
         nc.gpsimd.memset(scale_table[:, 2304:].bitcast(I32), 0)
         warm = sb.tile([P, 2], F32, name="warm")
@@ -66,18 +66,15 @@ def tile_picked_beamcell_none_p_kernel(tc, x_words, x_scales, w1, w2, w3, cell, 
         nc.gpsimd.memset(x_sc[:].bitcast(I32), 0)
 
         raw = {}
-        raw["i", 0] = load_w(w2, "i", 0)
+        raw["i", 0] = load_w(w2, "i", 0, "raw_i0")
         offsets = sb.tile([P, S // 16], U16, name="offsets")
         nc.sync.dma_start(offsets[:], offs)
-        raw["i", 1] = load_w(w2, "i", 1)
+        raw["i", 1] = load_w(w2, "i", 1, "raw_i1")
         nc.sync.dma_start(out=scale_table[4:P:8, :].bitcast(I32).rearrange("r (z c) -> r z c", z=PASSES),
                           in_=x_scales.bitcast(I32).rearrange("z r c -> r z c"))
         tables = [load_x(0)]
-        raw["g", 0] = load_w(w3, "g", 0)
+        raw["g", 0] = load_w(w3, "g", 0, "raw_g0")
         tables.append(load_x(1))
-        raw["g", 1] = load_w(w3, "g", 1)
-        for z in range(PASSES):
-            raw["f", z] = load_w(w1, "f", z)
 
         acc = {(gate, b): ps.tile([P, S], F32, name=f"acc_{gate}{b}") for gate in "gif" for b in range(BLOCKS)}
         x_codes = {}
@@ -109,30 +106,36 @@ def tile_picked_beamcell_none_p_kernel(tc, x_words, x_scales, w1, w2, w3, cell, 
         for z in range(PASSES):
             nc.vector.tensor_copy(picked_sc[:, z * S:(z + 1) * S], scale_table[:, z * T:(z + 1) * T].indirect(offsets[:]))
         for q in range(4):
-            nc.scalar.dma_start(out=x_sc[32 * q:32 * q + 4, :].bitcast(I32),
+            nc.sync.dma_start(out=x_sc[32 * q:32 * q + 4, :].bitcast(I32),
                                 in_=picked_sc[32 * q + 4:32 * q + 32:8, :].bitcast(I32))
+        raw["g", 1] = load_w(w3, "g", 1, "scale_table")
         wi = [whole("i", z, nc.scalar.copy) for z in range(PASSES)]
         gather_x(0)
+        raw["f", 0] = load_w(w1, "f", 0, "table0")
         wg = [whole("g", 0, nc.scalar.copy)]
+        raw["f", 1] = load_w(w1, "f", 1, "raw_g0")
         gather_x(1)
+        cells = [load_cell(0, "table1")]
         for z in range(PASSES):
             both("i", z, wi[z])
         for b in range(BLOCKS):
             activate("i", b, ACT.Sigmoid)
         wg.append(whole("g", 1, vcopy))
+        cells.append(load_cell(1, "scale_table"))
         for z in range(PASSES):
             both("g", z, wg[z])
         for b in range(BLOCKS):
             activate("g", b, ACT.Tanh)
         both("f", 0, whole("f", 0, vcopy))
         new = {}
-        for b, copy in enumerate((vcopy, vcopy)):
+        for b, copy in enumerate((vcopy, nc.scalar.copy)):
             codes, scales = quantize(interleave(copy, raw["f", 1], b * P, (b + 1) * P, f"bf_f1{b}"), P, f"f1{b}")
             multiply("f", b, 1, codes[:], scales[:])
             activate("f", b, ACT.Sigmoid)
-            new[b] = sb.tile([P, S], F32, name=f"new{b}")
+        new[0] = sb.tile([P, S], F32, name="new0", tag="bf_f10", align_bytes=64)
+        new[1] = sb.tile([P, S], F32, name="new1", tag="raw_g0")
+        for b in range(BLOCKS):
             nc.vector.tensor_tensor(new[b][:], act["i", b][:], act["g", b][:], ALU.mult)
-        cells = [load_cell(b) for b in range(BLOCKS)]
         for b, pieces in enumerate((1, 2)):
             H = S // pieces
             kept = [sb.tile([P, H], F32, name=f"kept{b}{h}") for h in range(pieces)]

@@ -28,18 +28,13 @@ def tile_picked_beamcell_none_p_kernel(tc, x_words, x_scales, w1, w2, w3, cell, 
         sb = ctx.enter_context(tc.tile_pool(name="sb", bufs=1))
         ps = ctx.enter_context(tc.psum_pool(name="ps", bufs=1))
 
-        def load_w(w, gate, z, tag):
-            raw = sb.tile([P, PACK, N], F32, name=f"raw_{gate}{z}", tag=tag)
-            nc.sync.dma_start(out=raw[:], in_=w[z * K_PASS:(z + 1) * K_PASS, :].rearrange("(p j) n -> p j n", j=PACK))
-            return raw
-
         def load_x(z):
             table = sb.tile([P, T], U32, name=f"words{z}", tag=f"table{z}")
             nc.sync.dma_start(out=table[:].bitcast(I32), in_=x_words[z].rearrange("p n t -> p (n t)").bitcast(I32))
             return table
 
-        def load_cell(b, tag):
-            rows = sb.tile([P, T], F32, name=f"cell{b}", tag=tag)
+        def load_cell(b):
+            rows = sb.tile([P, T], F32, name=f"cell{b}", tag=f"table{b}")
             nc.sync.dma_start(out=rows[:], in_=cell[b * P:(b + 1) * P, :])
             return rows
 
@@ -56,32 +51,40 @@ def tile_picked_beamcell_none_p_kernel(tc, x_words, x_scales, w1, w2, w3, cell, 
                                   in_=grouped[:].rearrange("p c t -> p (c t)"))
             return codes, scales
 
-        scale_table = sb.tile([P, PASSES * T], U8, name="scale_table", tag="scale_table")
-        nc.vector.memset(scale_table[:, :2304].bitcast(I32), 0)
-        nc.gpsimd.memset(scale_table[:, 2304:].bitcast(I32), 0)
+        scale_table = sb.tile([P, T], U8, name="scale_table", tag="first")
+        nc.sync.dma_start(out=scale_table[0:32, :].bitcast(I32), in_=x_scales.bitcast(I32).rearrange("z r c -> r z c"))
+        offsets = sb.tile([P, S // 16], U16, name="offsets")
+        nc.sync.dma_start(offsets[:], offs)
+        tables = [load_x(z) for z in range(PASSES)]
+        nc.vector.memset(scale_table[64:P, :].bitcast(I32), 0)
+        nc.gpsimd.memset(scale_table[32:64, :].bitcast(I32), 0)
         warm = sb.tile([P, 2], F32, name="warm")
         nc.vector.memset(warm[:, 0:1], 0.0)
         nc.scalar.activation(out=warm[:, 1:2], in_=warm[:, 0:1], func=ACT.Sigmoid)
         x_sc = sb.tile([P, PASSES * S], U8, name="x_sc", align_bytes=64)
         nc.gpsimd.memset(x_sc[:].bitcast(I32), 0)
 
+        picked_sc = sb.tile([P, S], U8, name="picked_sc")
+        nc.vector.tensor_copy(picked_sc[:], scale_table[:].indirect(offsets[:]))
+        for q in range(4):
+            nc.sync.dma_start(out=x_sc[32 * q:32 * q + 4, :].bitcast(I32).rearrange("s (z c) -> s z c", z=PASSES),
+                              in_=picked_sc[8 * q:8 * q + 8, :].bitcast(I32))
+
+        raw_all = sb.tile([P, 3 * PASSES * PACK * N], F32, name="raw_all", tag="first")
         raw = {}
-        raw["i", 0] = load_w(w2, "i", 0, "raw_i0")
-        offsets = sb.tile([P, S // 16], U16, name="offsets")
-        nc.sync.dma_start(offsets[:], offs)
-        raw["i", 1] = load_w(w2, "i", 1, "raw_i1")
-        nc.sync.dma_start(out=scale_table[4:P:8, :].bitcast(I32).rearrange("r (z c) -> r z c", z=PASSES),
-                          in_=x_scales.bitcast(I32).rearrange("z r c -> r z c"))
-        tables = [load_x(0)]
-        raw["g", 0] = load_w(w3, "g", 0, "raw_g0")
-        tables.append(load_x(1))
+        for g, (gate, w) in enumerate((("i", w2), ("g", w3), ("f", w1))):
+            for z in range(PASSES):
+                at = (g * PASSES + z) * PACK * N
+                raw[gate, z] = raw_all[:, at:at + PACK * N].rearrange("p (j n) -> p j n", j=PACK)
+                nc.sync.dma_start(out=raw[gate, z],
+                                  in_=w[z * K_PASS:(z + 1) * K_PASS, :].rearrange("(p j) n -> p j n", j=PACK))
 
         acc = {(gate, b): ps.tile([P, S], F32, name=f"acc_{gate}{b}") for gate in "gif" for b in range(BLOCKS)}
         x_codes = {}
-
-        def gather_x(z):
+        for z in range(PASSES):
             x_codes[z] = sb.tile([P, S], U32, name=f"x_codes{z}", align_bytes=64)
             nc.vector.tensor_copy(x_codes[z][:], tables[z][:].indirect(offsets[:]))
+        cells = [load_cell(b) for b in range(BLOCKS)]
 
         def multiply(gate, b, z, codes, scales):
             nc.tensor.matmul_mx(out=acc[gate, b][:], lhsT=codes.bitcast(FP8X4), lhsT_scale=scales,
@@ -89,9 +92,7 @@ def tile_picked_beamcell_none_p_kernel(tc, x_words, x_scales, w1, w2, w3, cell, 
                                 start=(z == 0), stop=(z == PASSES - 1))
 
         def whole(gate, z, copy):
-            return quantize(interleave(copy, raw[gate, z], 0, N, f"bf_{gate}{z}"), N, f"{gate}{z}")
-
-        def both(gate, z, pair):
+            pair = quantize(interleave(copy, raw[gate, z], 0, N, f"bf_{gate}{z}"), N, f"{gate}{z}")
             for b in range(BLOCKS):
                 multiply(gate, b, z, pair[0][:, b * P:(b + 1) * P], pair[1][:, b * P:(b + 1) * P])
 
@@ -102,39 +103,23 @@ def tile_picked_beamcell_none_p_kernel(tc, x_words, x_scales, w1, w2, w3, cell, 
             nc.scalar.activation(out=act[gate, b][:], in_=acc[gate, b][:], func=func)
 
         vcopy = nc.vector.tensor_copy
-        picked_sc = sb.tile([P, PASSES * S], U8, name="picked_sc")
-        for z in range(PASSES):
-            nc.vector.tensor_copy(picked_sc[:, z * S:(z + 1) * S], scale_table[:, z * T:(z + 1) * T].indirect(offsets[:]))
-        for q in range(4):
-            nc.sync.dma_start(out=x_sc[32 * q:32 * q + 4, :].bitcast(I32),
-                                in_=picked_sc[32 * q + 4:32 * q + 32:8, :].bitcast(I32))
-        raw["g", 1] = load_w(w3, "g", 1, "scale_table")
-        wi = [whole("i", z, nc.scalar.copy) for z in range(PASSES)]
-        gather_x(0)
-        raw["f", 0] = load_w(w1, "f", 0, "table0")
-        wg = [whole("g", 0, nc.scalar.copy)]
-        raw["f", 1] = load_w(w1, "f", 1, "raw_g0")
-        gather_x(1)
-        cells = [load_cell(0, "table1")]
-        for z in range(PASSES):
-            both("i", z, wi[z])
+        whole("i", 0, nc.scalar.copy)
+        whole("i", 1, nc.scalar.copy)
+        whole("g", 0, nc.scalar.copy)
         for b in range(BLOCKS):
             activate("i", b, ACT.Sigmoid)
-        wg.append(whole("g", 1, vcopy))
-        cells.append(load_cell(1, "scale_table"))
-        for z in range(PASSES):
-            both("g", z, wg[z])
+        whole("g", 1, vcopy)
         for b in range(BLOCKS):
             activate("g", b, ACT.Tanh)
-        both("f", 0, whole("f", 0, vcopy))
-        new = {}
-        for b, copy in enumerate((vcopy, nc.scalar.copy)):
-            codes, scales = quantize(interleave(copy, raw["f", 1], b * P, (b + 1) * P, f"bf_f1{b}"), P, f"f1{b}")
+        whole("f", 0, vcopy)
+        halves = [interleave(vcopy, raw["f", 1], b * P, (b + 1) * P, f"bf_f1{b}") for b in range(BLOCKS)]
+        for b in range(BLOCKS):
+            codes, scales = quantize(halves[b], P, f"f1{b}")
             multiply("f", b, 1, codes[:], scales[:])
             activate("f", b, ACT.Sigmoid)
-        new[0] = sb.tile([P, S], F32, name="new0", tag="bf_f10", align_bytes=64)
-        new[1] = sb.tile([P, S], F32, name="new1", tag="raw_g0")
+        new = {}
         for b in range(BLOCKS):
+            new[b] = sb.tile([P, S], F32, name=f"new{b}", tag=f"bf_f1{b}", align_bytes=64)
             nc.vector.tensor_tensor(new[b][:], act["i", b][:], act["g", b][:], ALU.mult)
         for b, pieces in enumerate((1, 2)):
             H = S // pieces

@@ -22,26 +22,39 @@ PASSES = K // K_PASS
 BLOCKS = N // P
 
 
+RAW_BYTES = PACK * N * 4
+
+
 def tile_picked_beamcell_none_p_kernel(tc, x_words, x_scales, w1, w2, w3, cell, offs, out):
     nc = tc.nc
     with ExitStack() as ctx:
         sb = ctx.enter_context(tc.tile_pool(name="sb", bufs=1))
+        stage = ctx.enter_context(tc.tile_pool(name="stage", bufs=1))
         ps = ctx.enter_context(tc.psum_pool(name="ps", bufs=1))
+        later = (("i", 1), ("g", 0), ("g", 1), ("f", 0), ("f", 1))
+        place = {key: n * RAW_BYTES for n, key in enumerate(later)}
+        weights = {"i": w2, "g": w3, "f": w1}
+        raw = {}
 
         def load_x(z):
             table = sb.tile([P, T], U32, name=f"words{z}", tag=f"table{z}")
             nc.sync.dma_start(out=table[:].bitcast(I32), in_=x_words[z].rearrange("p n t -> p (n t)").bitcast(I32))
             return table
 
+        def load_w(gate, z, room):
+            raw[gate, z] = room
+            nc.sync.dma_start(out=room[:], in_=weights[gate][z * K_PASS:(z + 1) * K_PASS, :].rearrange("(p j) n -> p j n", j=PACK))
+
         def load_cell(b):
             rows = sb.tile([P, T], F32, name=f"cell{b}", tag=f"table{b}")
             nc.sync.dma_start(out=rows[:], in_=cell[b * P:(b + 1) * P, :])
             return rows
 
-        def interleave(copy, raw, c0, c1, name):
+        def interleave(copy, gate, z, c0, c1):
+            name = f"bf_{gate}{z}_{c0}"
             grouped = sb.tile([P, c1 - c0, PACK], BF16, name=name, tag=name, align_bytes=64)
             copy(out=grouped[:].rearrange("p (c i) t -> p c t i", i=4),
-                 in_=raw[:, :, c0:c1].rearrange("p t (c i) -> p c t i", i=4))
+                 in_=raw[gate, z][:, :, c0:c1].rearrange("p t (c i) -> p c t i", i=4))
             return grouped
 
         def quantize(grouped, width, name):
@@ -51,13 +64,15 @@ def tile_picked_beamcell_none_p_kernel(tc, x_words, x_scales, w1, w2, w3, cell, 
                                   in_=grouped[:].rearrange("p c t -> p (c t)"))
             return codes, scales
 
-        scale_table = sb.tile([P, T], U8, name="scale_table", tag="first")
-        nc.sync.dma_start(out=scale_table[0:32, :].bitcast(I32), in_=x_scales.bitcast(I32).rearrange("z r c -> r z c"))
+        scale_table = stage.tile([P, len(later) * RAW_BYTES], U8, name="scale_table", offset=0)
+        nc.sync.dma_start(out=scale_table[0:32, :T].bitcast(I32), in_=x_scales.bitcast(I32).rearrange("z r c -> r z c"))
         offsets = sb.tile([P, S // 16], U16, name="offsets")
         nc.sync.dma_start(offsets[:], offs)
-        tables = [load_x(z) for z in range(PASSES)]
-        nc.vector.memset(scale_table[64:P, :].bitcast(I32), 0)
-        nc.gpsimd.memset(scale_table[32:64, :].bitcast(I32), 0)
+        tables = [load_x(0)]
+        load_w("i", 0, sb.tile([P, PACK, N], F32, name="raw_i0"))
+        tables.append(load_x(1))
+        nc.vector.memset(scale_table[64:P, :T].bitcast(I32), 0)
+        nc.gpsimd.memset(scale_table[32:64, :T].bitcast(I32), 0)
         warm = sb.tile([P, 2], F32, name="warm")
         nc.vector.memset(warm[:, 0:1], 0.0)
         nc.scalar.activation(out=warm[:, 1:2], in_=warm[:, 0:1], func=ACT.Sigmoid)
@@ -65,19 +80,12 @@ def tile_picked_beamcell_none_p_kernel(tc, x_words, x_scales, w1, w2, w3, cell, 
         nc.gpsimd.memset(x_sc[:].bitcast(I32), 0)
 
         picked_sc = sb.tile([P, S], U8, name="picked_sc")
-        nc.vector.tensor_copy(picked_sc[:], scale_table[:].indirect(offsets[:]))
+        nc.vector.tensor_copy(picked_sc[:], scale_table[:, :T].indirect(offsets[:]))
         for q in range(4):
             nc.sync.dma_start(out=x_sc[32 * q:32 * q + 4, :].bitcast(I32).rearrange("s (z c) -> s z c", z=PASSES),
                               in_=picked_sc[8 * q:8 * q + 8, :].bitcast(I32))
-
-        raw_all = sb.tile([P, 3 * PASSES * PACK * N], F32, name="raw_all", tag="first")
-        raw = {}
-        for g, (gate, w) in enumerate((("i", w2), ("g", w3), ("f", w1))):
-            for z in range(PASSES):
-                at = (g * PASSES + z) * PACK * N
-                raw[gate, z] = raw_all[:, at:at + PACK * N].rearrange("p (j n) -> p j n", j=PACK)
-                nc.sync.dma_start(out=raw[gate, z],
-                                  in_=w[z * K_PASS:(z + 1) * K_PASS, :].rearrange("(p j) n -> p j n", j=PACK))
+        for gate, z in later:
+            load_w(gate, z, stage.tile([P, PACK, N], F32, name=f"raw_{gate}{z}", offset=place[gate, z]))
 
         acc = {(gate, b): ps.tile([P, S], F32, name=f"acc_{gate}{b}") for gate in "gif" for b in range(BLOCKS)}
         x_codes = {}
@@ -92,42 +100,51 @@ def tile_picked_beamcell_none_p_kernel(tc, x_words, x_scales, w1, w2, w3, cell, 
                                 start=(z == 0), stop=(z == PASSES - 1))
 
         def whole(gate, z, copy):
-            pair = quantize(interleave(copy, raw[gate, z], 0, N, f"bf_{gate}{z}"), N, f"{gate}{z}")
+            pair = quantize(interleave(copy, gate, z, 0, N), N, f"{gate}{z}")
             for b in range(BLOCKS):
                 multiply(gate, b, z, pair[0][:, b * P:(b + 1) * P], pair[1][:, b * P:(b + 1) * P])
 
+        def halves(gate, z, copies):
+            grouped = [interleave(copy, gate, z, b * P, (b + 1) * P) for b, copy in enumerate(copies)]
+            for b in range(BLOCKS):
+                codes, scales = quantize(grouped[b], P, f"{gate}{z}{b}")
+                multiply(gate, b, z, codes[:], scales[:])
+
         act = {}
 
-        def activate(gate, b, func):
-            act[gate, b] = sb.tile([P, S], F32, name=f"act_{gate}{b}")
+        def activate(gate, b, func, after=None):
+            if after is None:
+                act[gate, b] = sb.tile([P, S], F32, name=f"act_{gate}{b}", align_bytes=64)
+            else:
+                act[gate, b] = stage.tile([P, S], F32, name=f"act_{gate}{b}", offset=place[after] + b * S * 4, align_bytes=64)
             nc.scalar.activation(out=act[gate, b][:], in_=acc[gate, b][:], func=func)
 
-        vcopy = nc.vector.tensor_copy
-        whole("i", 0, nc.scalar.copy)
-        whole("i", 1, nc.scalar.copy)
-        whole("g", 0, nc.scalar.copy)
+        vcopy, scopy = nc.vector.tensor_copy, nc.scalar.copy
+        whole("i", 0, scopy)
+        halves("i", 1, (vcopy, scopy))
+        halves("g", 0, (vcopy, scopy))
         for b in range(BLOCKS):
-            activate("i", b, ACT.Sigmoid)
+            activate("i", b, ACT.Sigmoid, ("g", 0))
         whole("g", 1, vcopy)
+        halves("f", 0, (vcopy, scopy))
         for b in range(BLOCKS):
-            activate("g", b, ACT.Tanh)
-        whole("f", 0, vcopy)
-        halves = [interleave(vcopy, raw["f", 1], b * P, (b + 1) * P, f"bf_f1{b}") for b in range(BLOCKS)]
-        for b in range(BLOCKS):
-            codes, scales = quantize(halves[b], P, f"f1{b}")
-            multiply("f", b, 1, codes[:], scales[:])
-            activate("f", b, ACT.Sigmoid)
+            activate("g", b, ACT.Tanh, ("f", 0))
+        grouped = [interleave(copy, "f", 1, b * P, (b + 1) * P) for b, copy in enumerate((vcopy, scopy))]
         new = {}
         for b in range(BLOCKS):
-            new[b] = sb.tile([P, S], F32, name=f"new{b}", tag=f"bf_f1{b}", align_bytes=64)
-            nc.vector.tensor_tensor(new[b][:], act["i", b][:], act["g", b][:], ALU.mult)
-        for b, pieces in enumerate((1, 2)):
-            H = S // pieces
-            kept = [sb.tile([P, H], F32, name=f"kept{b}{h}") for h in range(pieces)]
-            for h in range(pieces):
+            codes, scales = quantize(grouped[b], P, f"f1{b}")
+            multiply("f", b, 1, codes[:], scales[:])
+            activate("f", b, ACT.Sigmoid)
+            new[b] = raw["f", 1][:, :, b * P:(b + 1) * P]
+            nc.vector.tensor_tensor(new[b], act["i", b][:].rearrange("p (j c) -> p j c", j=PACK),
+                                    act["g", b][:].rearrange("p (j c) -> p j c", j=PACK), ALU.mult)
+        H = S // 2
+        for b in range(BLOCKS):
+            kept = [sb.tile([P, H], F32, name=f"kept{b}{h}") for h in range(2)]
+            for h in range(2):
                 nc.vector.tensor_tensor(kept[h][:], cells[b][:].indirect(offsets[:, h * H // 16:(h + 1) * H // 16]),
                                         act["f", b][:, h * H:(h + 1) * H], ALU.mult)
-            for h in range(pieces):
-                res = sb.tile([P, H], F32, name=f"res{b}{h}")
-                nc.vector.tensor_tensor(res[:], kept[h][:], new[b][:, h * H:(h + 1) * H], ALU.add)
-                nc.sync.dma_start(out=out[b * P:(b + 1) * P, h * H:(h + 1) * H], in_=res[:])
+            for h in range(2):
+                res = sb.tile([P, 2, P], F32, name=f"res{b}{h}")
+                nc.vector.tensor_tensor(res[:], kept[h][:].rearrange("p (j c) -> p j c", j=2), new[b][:, 2 * h:2 * h + 2, :], ALU.add)
+                nc.sync.dma_start(out=out[b * P:(b + 1) * P, h * H:(h + 1) * H], in_=res[:].rearrange("p j c -> p (j c)"))

@@ -81,8 +81,8 @@ def tile_picked_beamcell_none_p_kernel(tc, x_words, x_scales, w1, w2, w3, cell, 
 
         picked_sc = sb.tile([P, S], U8, name="picked_sc")
         nc.vector.tensor_copy(picked_sc[:], scale_table[:, :T].indirect(offsets[:]))
-        for q in range(4):
-            nc.sync.dma_start(out=x_sc[32 * q:32 * q + 4, :].bitcast(I32).rearrange("s (z c) -> s z c", z=PASSES),
+        for q in (0, 2, 1, 3):
+            nc.scalar.dma_start(out=x_sc[32 * q:32 * q + 4, :].bitcast(I32).rearrange("s (z c) -> s z c", z=PASSES),
                               in_=picked_sc[8 * q:8 * q + 8, :].bitcast(I32))
         for gate, z in later:
             load_w(gate, z, stage.tile([P, PACK, N], F32, name=f"raw_{gate}{z}", offset=place[gate, z]))

@@ -41,9 +41,9 @@ def tile_picked_beamcell_none_p_kernel(tc, x_words, x_scales, w1, w2, w3, cell, 
             nc.sync.dma_start(out=table[:].bitcast(I32), in_=x_words[z].rearrange("p n t -> p (n t)").bitcast(I32))
             return table
 
-        def load_w(gate, z, room):
+        def load_w(gate, z, room, queue):
             raw[gate, z] = room
-            nc.sync.dma_start(out=room[:], in_=weights[gate][z * K_PASS:(z + 1) * K_PASS, :].rearrange("(p j) n -> p j n", j=PACK))
+            queue.dma_start(out=room[:], in_=weights[gate][z * K_PASS:(z + 1) * K_PASS, :].rearrange("(p j) n -> p j n", j=PACK))
 
         def load_cell(b):
             rows = sb.tile([P, T], F32, name=f"cell{b}", tag=f"table{b}")
@@ -65,17 +65,14 @@ def tile_picked_beamcell_none_p_kernel(tc, x_words, x_scales, w1, w2, w3, cell, 
             return codes, scales
 
         scale_table = stage.tile([P, len(later) * RAW_BYTES], U8, name="scale_table", offset=0)
-        nc.sync.dma_start(out=scale_table[0:32, :T].bitcast(I32), in_=x_scales.bitcast(I32).rearrange("z r c -> r z c"))
+        nc.scalar.dma_start(out=scale_table[0:32, :T].bitcast(I32), in_=x_scales.bitcast(I32).rearrange("z r c -> r z c"))
         offsets = sb.tile([P, S // 16], U16, name="offsets")
         nc.sync.dma_start(offsets[:], offs)
         tables = [load_x(0)]
-        load_w("i", 0, sb.tile([P, PACK, N], F32, name="raw_i0"))
+        load_w("i", 0, sb.tile([P, PACK, N], F32, name="raw_i0"), nc.scalar)
         tables.append(load_x(1))
         nc.vector.memset(scale_table[64:P, :T].bitcast(I32), 0)
         nc.gpsimd.memset(scale_table[32:64, :T].bitcast(I32), 0)
-        warm = sb.tile([P, 2], F32, name="warm")
-        nc.vector.memset(warm[:, 0:1], 0.0)
-        nc.scalar.activation(out=warm[:, 1:2], in_=warm[:, 0:1], func=ACT.Sigmoid)
         x_sc = sb.tile([P, PASSES * S], U8, name="x_sc", align_bytes=64)
         nc.gpsimd.memset(x_sc[:].bitcast(I32), 0)
 
@@ -85,7 +82,7 @@ def tile_picked_beamcell_none_p_kernel(tc, x_words, x_scales, w1, w2, w3, cell, 
             nc.scalar.dma_start(out=x_sc[32 * q:32 * q + 4, :].bitcast(I32).rearrange("s (z c) -> s z c", z=PASSES),
                               in_=picked_sc[8 * q:8 * q + 8, :].bitcast(I32))
         for gate, z in later:
-            load_w(gate, z, stage.tile([P, PACK, N], F32, name=f"raw_{gate}{z}", offset=place[gate, z]))
+            load_w(gate, z, stage.tile([P, PACK, N], F32, name=f"raw_{gate}{z}", offset=place[gate, z]), nc.sync)
 
         acc = {(gate, b): ps.tile([P, S], F32, name=f"acc_{gate}{b}") for gate in "gif" for b in range(BLOCKS)}
         x_codes = {}
@@ -120,12 +117,12 @@ def tile_picked_beamcell_none_p_kernel(tc, x_words, x_scales, w1, w2, w3, cell, 
             nc.scalar.activation(out=act[gate, b][:], in_=acc[gate, b][:], func=func)
 
         vcopy, scopy = nc.vector.tensor_copy, nc.scalar.copy
-        whole("i", 0, scopy)
-        halves("i", 1, (vcopy, scopy))
-        halves("g", 0, (vcopy, scopy))
+        for z in range(PASSES):
+            whole("i", z, vcopy)
         for b in range(BLOCKS):
-            activate("i", b, ACT.Sigmoid, ("g", 0))
-        whole("g", 1, vcopy)
+            activate("i", b, ACT.Sigmoid)
+        for z in range(PASSES):
+            whole("g", z, vcopy)
         halves("f", 0, (vcopy, scopy))
         for b in range(BLOCKS):
             activate("g", b, ACT.Tanh, ("f", 0))
@@ -147,4 +144,4 @@ def tile_picked_beamcell_none_p_kernel(tc, x_words, x_scales, w1, w2, w3, cell, 
             for h in range(2):
                 res = sb.tile([P, 2, P], F32, name=f"res{b}{h}")
                 nc.vector.tensor_tensor(res[:], kept[h][:].rearrange("p (j c) -> p j c", j=2), new[b][:, 2 * h:2 * h + 2, :], ALU.add)
-                nc.sync.dma_start(out=out[b * P:(b + 1) * P, h * H:(h + 1) * H], in_=res[:].rearrange("p j c -> p (j c)"))
+                (nc.sync, nc.scalar)[h].dma_start(out=out[b * P:(b + 1) * P, h * H:(h + 1) * H], in_=res[:].rearrange("p j c -> p (j c)"))

@@ -19,10 +19,16 @@ P = 128
 PACK = 4
 K_PASS = P * PACK
 PASSES = K // K_PASS
-BLOCKS = N // P
-
-
+HALVES = N // P
+QUADRANT = 32
+SCALE_ROWS = K // 32
+ROWS_IN_QUADRANT = 4
+LIST_GROUP = 16
+LINE = 4
 RAW_BYTES = PACK * N * 4
+ACT_BYTES = S * 4
+PIECES = 2
+PIECE = S // PIECES
 
 
 def tile_picked_beamcell_none_p_kernel(tc, x_words, x_scales, w1, w2, w3, cell, offs, out):
@@ -31,30 +37,31 @@ def tile_picked_beamcell_none_p_kernel(tc, x_words, x_scales, w1, w2, w3, cell, 
         sb = ctx.enter_context(tc.tile_pool(name="sb", bufs=1))
         stage = ctx.enter_context(tc.tile_pool(name="stage", bufs=1))
         ps = ctx.enter_context(tc.psum_pool(name="ps", bufs=1))
-        later = (("i", 1), ("g", 0), ("g", 1), ("f", 0), ("f", 1))
-        place = {key: n * RAW_BYTES for n, key in enumerate(later)}
+
+        staged = (("i", 1), ("g", 0), ("g", 1), ("f", 0), ("f", 1))
+        place = {key: n * RAW_BYTES for n, key in enumerate(staged)}
         weights = {"i": w2, "g": w3, "f": w1}
         raw = {}
 
-        def load_x(z):
+        def load_words(z):
             table = sb.tile([P, T], U32, name=f"words{z}", tag=f"table{z}")
             nc.sync.dma_start(out=table[:].bitcast(I32), in_=x_words[z].rearrange("p n t -> p (n t)").bitcast(I32))
             return table
 
-        def load_w(gate, z, room, queue):
+        def load_weights(gate, z, room, queue):
             raw[gate, z] = room
-            queue.dma_start(out=room[:], in_=weights[gate][z * K_PASS:(z + 1) * K_PASS, :].rearrange("(p j) n -> p j n", j=PACK))
+            k_rows = slice(z * K_PASS, (z + 1) * K_PASS)
+            queue.dma_start(out=room[:], in_=weights[gate][k_rows, :].rearrange("(p j) n -> p j n", j=PACK))
 
-        def load_cell(b):
-            rows = sb.tile([P, T], F32, name=f"cell{b}", tag=f"table{b}")
-            nc.sync.dma_start(out=rows[:], in_=cell[b * P:(b + 1) * P, :])
+        def load_cell(half):
+            rows = sb.tile([P, T], F32, name=f"cell{half}", tag=f"table{half}")
+            nc.sync.dma_start(out=rows[:], in_=cell[half * P:(half + 1) * P, :])
             return rows
 
         def interleave(copy, gate, z, c0, c1):
-            name = f"bf_{gate}{z}_{c0}"
-            grouped = sb.tile([P, c1 - c0, PACK], BF16, name=name, tag=name, align_bytes=64)
-            copy(out=grouped[:].rearrange("p (c i) t -> p c t i", i=4),
-                 in_=raw[gate, z][:, :, c0:c1].rearrange("p t (c i) -> p c t i", i=4))
+            grouped = sb.tile([P, c1 - c0, PACK], BF16, name=f"bf_{gate}{z}_{c0}", align_bytes=64)
+            copy(out=grouped[:].rearrange("p (c i) t -> p c t i", i=LINE),
+                 in_=raw[gate, z][:, :, c0:c1].rearrange("p t (c i) -> p c t i", i=LINE))
             return grouped
 
         def quantize(grouped, width, name):
@@ -64,84 +71,94 @@ def tile_picked_beamcell_none_p_kernel(tc, x_words, x_scales, w1, w2, w3, cell, 
                                   in_=grouped[:].rearrange("p c t -> p (c t)"))
             return codes, scales
 
-        scale_table = stage.tile([P, len(later) * RAW_BYTES], U8, name="scale_table", offset=0)
-        nc.scalar.dma_start(out=scale_table[0:32, :T].bitcast(I32), in_=x_scales.bitcast(I32).rearrange("z r c -> r z c"))
-        offsets = sb.tile([P, S // 16], U16, name="offsets")
+        scale_table = stage.tile([P, len(staged) * RAW_BYTES], U8, name="scale_table", offset=0)
+        nc.scalar.dma_start(out=scale_table[0:SCALE_ROWS, :T].bitcast(I32),
+                            in_=x_scales.bitcast(I32).rearrange("z r c -> r z c"))
+        offsets = sb.tile([P, S // LIST_GROUP], U16, name="offsets")
         nc.sync.dma_start(offsets[:], offs)
-        tables = [load_x(0)]
-        load_w("i", 0, sb.tile([P, PACK, N], F32, name="raw_i0"), nc.scalar)
-        tables.append(load_x(1))
-        nc.vector.memset(scale_table[64:P, :T].bitcast(I32), 0)
-        nc.gpsimd.memset(scale_table[32:64, :T].bitcast(I32), 0)
+        tables = [load_words(0)]
+        load_weights("i", 0, sb.tile([P, PACK, N], F32, name="raw_i0"), nc.scalar)
+        tables.append(load_words(1))
+        nc.vector.memset(scale_table[2 * QUADRANT:P, :T].bitcast(I32), 0)
+        nc.gpsimd.memset(scale_table[QUADRANT:2 * QUADRANT, :T].bitcast(I32), 0)
+
         x_sc = sb.tile([P, PASSES * S], U8, name="x_sc", align_bytes=64)
         nc.gpsimd.memset(x_sc[:].bitcast(I32), 0)
-
         picked_sc = sb.tile([P, S], U8, name="picked_sc")
         nc.vector.tensor_copy(picked_sc[:], scale_table[:, :T].indirect(offsets[:]))
+        picked_rows = ROWS_IN_QUADRANT * PASSES
         for q in (0, 2, 1, 3):
-            nc.scalar.dma_start(out=x_sc[32 * q:32 * q + 4, :].bitcast(I32).rearrange("s (z c) -> s z c", z=PASSES),
-                              in_=picked_sc[8 * q:8 * q + 8, :].bitcast(I32))
-        for gate, z in later:
-            load_w(gate, z, stage.tile([P, PACK, N], F32, name=f"raw_{gate}{z}", offset=place[gate, z]), nc.sync)
+            nc.scalar.dma_start(
+                out=x_sc[QUADRANT * q:QUADRANT * q + ROWS_IN_QUADRANT, :].bitcast(I32).rearrange("s (z c) -> s z c", z=PASSES),
+                in_=picked_sc[picked_rows * q:picked_rows * (q + 1), :].bitcast(I32))
+        for gate, z in staged:
+            load_weights(gate, z, stage.tile([P, PACK, N], F32, name=f"raw_{gate}{z}", offset=place[gate, z]), nc.sync)
 
-        acc = {(gate, b): ps.tile([P, S], F32, name=f"acc_{gate}{b}") for gate in "gif" for b in range(BLOCKS)}
+        acc = {(gate, half): ps.tile([P, S], F32, name=f"acc_{gate}{half}") for gate in "gif" for half in range(HALVES)}
         x_codes = {}
         for z in range(PASSES):
             x_codes[z] = sb.tile([P, S], U32, name=f"x_codes{z}", align_bytes=64)
             nc.vector.tensor_copy(x_codes[z][:], tables[z][:].indirect(offsets[:]))
-        cells = [load_cell(b) for b in range(BLOCKS)]
+        cells = [load_cell(half) for half in range(HALVES)]
 
-        def multiply(gate, b, z, codes, scales):
-            nc.tensor.matmul_mx(out=acc[gate, b][:], lhsT=codes.bitcast(FP8X4), lhsT_scale=scales,
+        def multiply(gate, half, z, codes, scales):
+            nc.tensor.matmul_mx(out=acc[gate, half][:], lhsT=codes.bitcast(FP8X4), lhsT_scale=scales,
                                 rhs=x_codes[z][:].bitcast(FP8X4), rhs_scale=x_sc[:, z * S:(z + 1) * S],
                                 start=(z == 0), stop=(z == PASSES - 1))
 
-        def whole(gate, z, copy):
-            pair = quantize(interleave(copy, gate, z, 0, N), N, f"{gate}{z}")
-            for b in range(BLOCKS):
-                multiply(gate, b, z, pair[0][:, b * P:(b + 1) * P], pair[1][:, b * P:(b + 1) * P])
+        def whole_pass(gate, z):
+            codes, scales = quantize(interleave(nc.vector.tensor_copy, gate, z, 0, N), N, f"{gate}{z}")
+            for half in range(HALVES):
+                cols = slice(half * P, (half + 1) * P)
+                multiply(gate, half, z, codes[:, cols], scales[:, cols])
 
-        def halves(gate, z, copies):
-            grouped = [interleave(copy, gate, z, b * P, (b + 1) * P) for b, copy in enumerate(copies)]
-            for b in range(BLOCKS):
-                codes, scales = quantize(grouped[b], P, f"{gate}{z}{b}")
-                multiply(gate, b, z, codes[:], scales[:])
+        def shared_cast(gate, z):
+            return [interleave(copy, gate, z, half * P, (half + 1) * P)
+                    for half, copy in enumerate((nc.vector.tensor_copy, nc.scalar.copy))]
+
+        def half_pass(gate, half, z, grouped):
+            codes, scales = quantize(grouped, P, f"{gate}{z}{half}")
+            multiply(gate, half, z, codes[:], scales[:])
 
         act = {}
 
-        def activate(gate, b, func, after=None):
-            if after is None:
-                act[gate, b] = sb.tile([P, S], F32, name=f"act_{gate}{b}", align_bytes=64)
-            else:
-                act[gate, b] = stage.tile([P, S], F32, name=f"act_{gate}{b}", offset=place[after] + b * S * 4, align_bytes=64)
-            nc.scalar.activation(out=act[gate, b][:], in_=acc[gate, b][:], func=func)
+        def activate(gate, half, func, room):
+            act[gate, half] = room
+            nc.scalar.activation(out=room[:], in_=acc[gate, half][:], func=func)
 
-        vcopy, scopy = nc.vector.tensor_copy, nc.scalar.copy
         for z in range(PASSES):
-            whole("i", z, vcopy)
-        for b in range(BLOCKS):
-            activate("i", b, ACT.Sigmoid)
+            whole_pass("i", z)
+        for half in range(HALVES):
+            activate("i", half, ACT.Sigmoid, sb.tile([P, S], F32, name=f"act_i{half}", align_bytes=64))
         for z in range(PASSES):
-            whole("g", z, vcopy)
-        halves("f", 0, (vcopy, scopy))
-        for b in range(BLOCKS):
-            activate("g", b, ACT.Tanh, ("f", 0))
-        grouped = [interleave(copy, "f", 1, b * P, (b + 1) * P) for b, copy in enumerate((vcopy, scopy))]
+            whole_pass("g", z)
+        grouped = shared_cast("f", 0)
+        for half in range(HALVES):
+            half_pass("f", half, 0, grouped[half])
+        for half in range(HALVES):
+            activate("g", half, ACT.Tanh, stage.tile([P, S], F32, name=f"act_g{half}",
+                                                     offset=place["f", 0] + half * ACT_BYTES, align_bytes=64))
+        grouped = shared_cast("f", 1)
         new = {}
-        for b in range(BLOCKS):
-            codes, scales = quantize(grouped[b], P, f"f1{b}")
-            multiply("f", b, 1, codes[:], scales[:])
-            activate("f", b, ACT.Sigmoid)
-            new[b] = raw["f", 1][:, :, b * P:(b + 1) * P]
-            nc.vector.tensor_tensor(new[b], act["i", b][:].rearrange("p (j c) -> p j c", j=PACK),
-                                    act["g", b][:].rearrange("p (j c) -> p j c", j=PACK), ALU.mult)
-        H = S // 2
-        for b in range(BLOCKS):
-            kept = [sb.tile([P, H], F32, name=f"kept{b}{h}") for h in range(2)]
-            for h in range(2):
-                nc.vector.tensor_tensor(kept[h][:], cells[b][:].indirect(offsets[:, h * H // 16:(h + 1) * H // 16]),
-                                        act["f", b][:, h * H:(h + 1) * H], ALU.mult)
-            for h in range(2):
-                res = sb.tile([P, 2, P], F32, name=f"res{b}{h}")
-                nc.vector.tensor_tensor(res[:], kept[h][:].rearrange("p (j c) -> p j c", j=2), new[b][:, 2 * h:2 * h + 2, :], ALU.add)
-                (nc.sync, nc.scalar)[h].dma_start(out=out[b * P:(b + 1) * P, h * H:(h + 1) * H], in_=res[:].rearrange("p j c -> p (j c)"))
+        for half in range(HALVES):
+            half_pass("f", half, 1, grouped[half])
+            activate("f", half, ACT.Sigmoid, sb.tile([P, S], F32, name=f"act_f{half}", align_bytes=64))
+            new[half] = raw["f", 1][:, :, half * P:(half + 1) * P]
+            nc.vector.tensor_tensor(new[half], act["i", half][:].rearrange("p (run c) -> p run c", c=P),
+                                    act["g", half][:].rearrange("p (run c) -> p run c", c=P), ALU.mult)
+
+        runs = PIECE // P
+        for half in range(HALVES):
+            kept = [sb.tile([P, PIECE], F32, name=f"kept{half}{piece}") for piece in range(PIECES)]
+            for piece in range(PIECES):
+                entries = offsets[:, piece * PIECE // LIST_GROUP:(piece + 1) * PIECE // LIST_GROUP]
+                nc.vector.tensor_tensor(kept[piece][:], cells[half][:].indirect(entries),
+                                        act["f", half][:, piece * PIECE:(piece + 1) * PIECE], ALU.mult)
+            for piece in range(PIECES):
+                res = sb.tile([P, runs, P], F32, name=f"res{half}{piece}")
+                nc.vector.tensor_tensor(res[:], kept[piece][:].rearrange("p (run c) -> p run c", c=P),
+                                        new[half][:, runs * piece:runs * (piece + 1), :], ALU.add)
+                last = half == HALVES - 1 and piece == PIECES - 1
+                (nc.scalar if last else nc.sync).dma_start(
+                    out=out[half * P:(half + 1) * P, piece * PIECE:(piece + 1) * PIECE],
+                    in_=res[:].rearrange("p run c -> p (run c)"))

@@ -158,7 +158,5 @@ def tile_picked_beamcell_none_p_kernel(tc, x_words, x_scales, w1, w2, w3, cell, 
                 res = sb.tile([P, runs, P], F32, name=f"res{half}{piece}")
                 nc.vector.tensor_tensor(res[:], kept[piece][:].rearrange("p (run c) -> p run c", c=P),
                                         new[half][:, runs * piece:runs * (piece + 1), :], ALU.add)
-                last = half == HALVES - 1 and piece == PIECES - 1
-                (nc.scalar if last else nc.sync).dma_start(
-                    out=out[half * P:(half + 1) * P, piece * PIECE:(piece + 1) * PIECE],
-                    in_=res[:].rearrange("p run c -> p (run c)"))
+                nc.sync.dma_start(out=out[half * P:(half + 1) * P, piece * PIECE:(piece + 1) * PIECE],
+                                  in_=res[:].rearrange("p run c -> p (run c)"))

@@ -59,13 +59,14 @@ def tile_picked_beamcell_none_p_kernel(tc, x_words, x_scales, w1, w2, w3, cell, 
             return rows
 
         def interleave(copy, gate, z, c0, c1):
-            grouped = sb.tile([P, c1 - c0, PACK], BF16, name=f"bf_{gate}{z}_{c0}", align_bytes=64)
+            grouped = sb.tile([P, c1 - c0, PACK], BF16, name=f"bf_{gate}{z}_{c0}",
+                              tag="codes_g11" if (gate, z, c0) == ("f", 1, P) else f"bf_{gate}{z}_{c0}", align_bytes=64)
             copy(out=grouped[:].rearrange("p (c i) t -> p c t i", i=LINE),
                  in_=raw[gate, z][:, :, c0:c1].rearrange("p t (c i) -> p c t i", i=LINE))
             return grouped
 
-        def quantize(grouped, width, name):
-            codes = sb.tile([P, width], U32, name=f"codes_{name}", align_bytes=64)
+        def quantize(grouped, width, name, room=None):
+            codes = room or sb.tile([P, width], U32, name=f"codes_{name}", align_bytes=64)
             scales = sb.tile([P, width], U8, name=f"scales_{name}", align_bytes=64)
             nc.vector.quantize_mx(out=codes[:].bitcast(FP8X4), scales=scales[:],
                                   in_=grouped[:].rearrange("p c t -> p (c t)"))
@@ -88,37 +89,42 @@ def tile_picked_beamcell_none_p_kernel(tc, x_words, x_scales, w1, w2, w3, cell, 
         nc.vector.tensor_copy(picked_sc[:], scale_table[:, :T].indirect(offsets[:]))
         picked_rows = ROWS_IN_QUADRANT * PASSES
         for q in (0, 2, 1, 3):
-            nc.scalar.dma_start(
+            nc.sync.dma_start(
                 out=x_sc[QUADRANT * q:QUADRANT * q + ROWS_IN_QUADRANT, :].bitcast(I32).rearrange("s (z c) -> s z c", z=PASSES),
                 in_=picked_sc[picked_rows * q:picked_rows * (q + 1), :].bitcast(I32))
         for gate, z in staged:
             load_weights(gate, z, stage.tile([P, PACK, N], F32, name=f"raw_{gate}{z}", offset=place[gate, z]), nc.sync)
 
-        acc = {(gate, half): ps.tile([P, S], F32, name=f"acc_{gate}{half}") for gate in "gif" for half in range(HALVES)}
+        acc = {(gate, half): ps.tile([P, S], F32, name=f"acc_{gate}{half}")
+               for gate in "gif" for half in range(HALVES) if (gate, half) != ("f", 0)}
+        acc_first = [ps.tile([P, PIECE], F32, name=f"acc_f0{piece}") for piece in range(PIECES)]
         x_codes = {}
         for z in range(PASSES):
             x_codes[z] = sb.tile([P, S], U32, name=f"x_codes{z}", align_bytes=64)
             nc.vector.tensor_copy(x_codes[z][:], tables[z][:].indirect(offsets[:]))
         cells = [load_cell(half) for half in range(HALVES)]
 
-        def multiply(gate, half, z, codes, scales):
-            nc.tensor.matmul_mx(out=acc[gate, half][:], lhsT=codes.bitcast(FP8X4), lhsT_scale=scales,
-                                rhs=x_codes[z][:].bitcast(FP8X4), rhs_scale=x_sc[:, z * S:(z + 1) * S],
+        def multiply(sums, z, codes, scales, j0=0, j1=S):
+            nc.tensor.matmul_mx(out=sums, lhsT=codes.bitcast(FP8X4), lhsT_scale=scales,
+                                rhs=x_codes[z][:, j0:j1].bitcast(FP8X4), rhs_scale=x_sc[:, z * S + j0:z * S + j1],
                                 start=(z == 0), stop=(z == PASSES - 1))
 
         def whole_pass(gate, z):
             codes, scales = quantize(interleave(nc.vector.tensor_copy, gate, z, 0, N), N, f"{gate}{z}")
             for half in range(HALVES):
                 cols = slice(half * P, (half + 1) * P)
-                multiply(gate, half, z, codes[:, cols], scales[:, cols])
+                multiply(acc[gate, half][:], z, codes[:, cols], scales[:, cols])
 
-        def shared_cast(gate, z):
-            return [interleave(copy, gate, z, half * P, (half + 1) * P)
-                    for half, copy in enumerate((nc.vector.tensor_copy, nc.scalar.copy))]
+        def cast_halves(gate, z, copies):
+            return [interleave(copy, gate, z, half * P, (half + 1) * P) for half, copy in enumerate(copies)]
 
-        def half_pass(gate, half, z, grouped):
-            codes, scales = quantize(grouped, P, f"{gate}{z}{half}")
-            multiply(gate, half, z, codes[:], scales[:])
+        def half_pass(gate, half, z, grouped, room=None):
+            codes, scales = quantize(grouped, P, f"{gate}{z}{half}", room)
+            if (gate, half) == ("f", 0):
+                for piece in range(PIECES):
+                    multiply(acc_first[piece][:], z, codes[:], scales[:], piece * PIECE, (piece + 1) * PIECE)
+            else:
+                multiply(acc[gate, half][:], z, codes[:], scales[:])
 
         act = {}
 
@@ -126,26 +132,35 @@ def tile_picked_beamcell_none_p_kernel(tc, x_words, x_scales, w1, w2, w3, cell, 
             act[gate, half] = room
             nc.scalar.activation(out=room[:], in_=acc[gate, half][:], func=func)
 
-        for z in range(PASSES):
-            whole_pass("i", z)
+        shared = (nc.vector.tensor_copy, nc.scalar.copy)
+        whole_pass("i", 0)
+        grouped = cast_halves("i", 1, (nc.vector.tensor_copy, nc.vector.tensor_copy))
+        for half in range(HALVES):
+            half_pass("i", half, 1, grouped[half])
         for half in range(HALVES):
             activate("i", half, ACT.Sigmoid, sb.tile([P, S], F32, name=f"act_i{half}", align_bytes=64))
-        for z in range(PASSES):
-            whole_pass("g", z)
-        grouped = shared_cast("f", 0)
+        whole_pass("g", 0)
+        grouped = cast_halves("g", 1, (nc.vector.tensor_copy, nc.vector.tensor_copy))
         for half in range(HALVES):
+            half_pass("g", half, 1, grouped[half])
+        grouped = cast_halves("f", 0, shared)
+        for half in reversed(range(HALVES)):
             half_pass("f", half, 0, grouped[half])
         for half in range(HALVES):
             activate("g", half, ACT.Tanh, stage.tile([P, S], F32, name=f"act_g{half}",
                                                      offset=place["f", 0] + half * ACT_BYTES, align_bytes=64))
-        grouped = shared_cast("f", 1)
+        grouped = cast_halves("f", 1, shared)
+        half_pass("f", 0, 1, grouped[0])
+        act["f", 0] = sb.tile([P, S], F32, name="act_f0", align_bytes=64)
+        for piece in range(PIECES):
+            nc.scalar.activation(out=act["f", 0][:, piece * PIECE:(piece + 1) * PIECE], in_=acc_first[piece][:], func=ACT.Sigmoid)
         new = {}
         for half in range(HALVES):
-            half_pass("f", half, 1, grouped[half])
-            activate("f", half, ACT.Sigmoid, sb.tile([P, S], F32, name=f"act_f{half}", align_bytes=64))
-            new[half] = raw["f", 1][:, :, half * P:(half + 1) * P]
+            new[half] = raw["f", 1][:, :, :P] if half == 0 else sb.tile([P, PACK, P], F32, name="new1")[:]
             nc.vector.tensor_tensor(new[half], act["i", half][:].rearrange("p (run c) -> p run c", c=P),
                                     act["g", half][:].rearrange("p (run c) -> p run c", c=P), ALU.mult)
+        half_pass("f", 1, 1, grouped[1], stage.tile([P, P], U32, name="codes_f11", offset=place["f", 0], align_bytes=64))
+        activate("f", 1, ACT.Sigmoid, sb.tile([P, S], F32, name="act_f1", align_bytes=64))
 
         runs = PIECE // P
         for half in range(HALVES):

@@ -26,9 +26,10 @@ ROWS_IN_QUADRANT = 4
 LIST_GROUP = 16
 LINE = 4
 RAW_BYTES = PACK * N * 4
-ACT_BYTES = S * 4
+ROW_BYTES = T * 4
 PIECES = 2
 PIECE = S // PIECES
+RUNS = S // P
 
 
 def tile_picked_beamcell_none_p_kernel(tc, x_words, x_scales, w1, w2, w3, cell, offs, out):
@@ -38,53 +39,59 @@ def tile_picked_beamcell_none_p_kernel(tc, x_words, x_scales, w1, w2, w3, cell, 
         stage = ctx.enter_context(tc.tile_pool(name="stage", bufs=1))
         ps = ctx.enter_context(tc.psum_pool(name="ps", bufs=1))
 
-        staged = (("i", 1), ("g", 0), ("g", 1), ("f", 0), ("f", 1))
-        place = {key: n * RAW_BYTES for n, key in enumerate(staged)}
         weights = {"i": w2, "g": w3, "f": w1}
+        late_passes = (("g", 1), ("f", 0), ("f", 1))
+        late_bytes = len(late_passes) * RAW_BYTES
+        held_bytes = late_bytes + ROW_BYTES
+        table_place = (held_bytes, late_bytes)
         raw = {}
 
         def load_words(z):
-            table = sb.tile([P, T], U32, name=f"words{z}", tag=f"table{z}")
+            table = stage.tile([P, T], U32, name=f"words{z}", offset=table_place[z])
             nc.sync.dma_start(out=table[:].bitcast(I32), in_=x_words[z].rearrange("p n t -> p (n t)").bitcast(I32))
             return table
 
-        def load_weights(gate, z, room, queue):
+        def load_pass(gate, z, room):
             raw[gate, z] = room
             k_rows = slice(z * K_PASS, (z + 1) * K_PASS)
-            queue.dma_start(out=room[:], in_=weights[gate][k_rows, :].rearrange("(p j) n -> p j n", j=PACK))
+            nc.sync.dma_start(out=room[:], in_=weights[gate][k_rows, :].rearrange("(p t) n -> p t n", t=PACK))
 
         def load_cell(half):
-            rows = sb.tile([P, T], F32, name=f"cell{half}", tag=f"table{half}")
+            rows = stage.tile([P, T], F32, name=f"cell{half}", offset=table_place[half])
             nc.sync.dma_start(out=rows[:], in_=cell[half * P:(half + 1) * P, :])
             return rows
 
-        def interleave(copy, gate, z, c0, c1):
-            grouped = sb.tile([P, c1 - c0, PACK], BF16, name=f"bf_{gate}{z}_{c0}",
-                              tag="codes_g11" if (gate, z, c0) == ("f", 1, P) else f"bf_{gate}{z}_{c0}", align_bytes=64)
+        def interleave(copy, gate, z, c0, c1, tag=None):
+            name = f"bf_{gate}{z}_{c0}"
+            grouped = sb.tile([P, c1 - c0, PACK], BF16, name=name, tag=tag or name, align_bytes=64)
             copy(out=grouped[:].rearrange("p (c i) t -> p c t i", i=LINE),
                  in_=raw[gate, z][:, :, c0:c1].rearrange("p t (c i) -> p c t i", i=LINE))
             return grouped
 
-        def quantize(grouped, width, name, room=None):
-            codes = room or sb.tile([P, width], U32, name=f"codes_{name}", align_bytes=64)
+        def quantize(grouped, width, name, tag=None):
+            codes = sb.tile([P, width], U32, name=f"codes_{name}", tag=tag or f"codes_{name}", align_bytes=64)
             scales = sb.tile([P, width], U8, name=f"scales_{name}", align_bytes=64)
             nc.vector.quantize_mx(out=codes[:].bitcast(FP8X4), scales=scales[:],
                                   in_=grouped[:].rearrange("p c t -> p (c t)"))
             return codes, scales
 
-        scale_table = stage.tile([P, len(staged) * RAW_BYTES], U8, name="scale_table", offset=0)
-        nc.scalar.dma_start(out=scale_table[0:SCALE_ROWS, :T].bitcast(I32),
-                            in_=x_scales.bitcast(I32).rearrange("z r c -> r z c"))
+        scale_table = stage.tile([P, held_bytes], U8, name="scale_table", offset=0)
+        nc.sync.dma_start(out=scale_table[0:SCALE_ROWS, :T].bitcast(I32),
+                          in_=x_scales.bitcast(I32).rearrange("z r c -> r z c"))
         offsets = sb.tile([P, S // LIST_GROUP], U16, name="offsets")
         nc.sync.dma_start(offsets[:], offs)
         tables = [load_words(0)]
-        load_weights("i", 0, sb.tile([P, PACK, N], F32, name="raw_i0"), nc.scalar)
-        tables.append(load_words(1))
+        raw_i = sb.tile([P, PASSES, PACK, N], F32, name="raw_i")
+        nc.sync.dma_start(out=raw_i[:].rearrange("p z t n -> p z (t n)"),
+                          in_=weights["i"].rearrange("(z p t) n -> p z (t n)", p=P, t=PACK))
+        for z in range(PASSES):
+            raw["i", z] = raw_i[:, z]
+        load_pass("g", 0, sb.tile([P, PACK, N], F32, name="raw_g0"))
         nc.vector.memset(scale_table[2 * QUADRANT:P, :T].bitcast(I32), 0)
-        nc.gpsimd.memset(scale_table[QUADRANT:2 * QUADRANT, :T].bitcast(I32), 0)
+        nc.vector.memset(scale_table[QUADRANT:2 * QUADRANT, :T].bitcast(I32), 0)
 
         x_sc = sb.tile([P, PASSES * S], U8, name="x_sc", align_bytes=64)
-        nc.gpsimd.memset(x_sc[:].bitcast(I32), 0)
+        nc.vector.memset(x_sc[:].bitcast(I32), 0)
         picked_sc = sb.tile([P, S], U8, name="picked_sc")
         nc.vector.tensor_copy(picked_sc[:], scale_table[:, :T].indirect(offsets[:]))
         picked_rows = ROWS_IN_QUADRANT * PASSES
@@ -92,77 +99,72 @@ def tile_picked_beamcell_none_p_kernel(tc, x_words, x_scales, w1, w2, w3, cell, 
             nc.sync.dma_start(
                 out=x_sc[QUADRANT * q:QUADRANT * q + ROWS_IN_QUADRANT, :].bitcast(I32).rearrange("s (z c) -> s z c", z=PASSES),
                 in_=picked_sc[picked_rows * q:picked_rows * (q + 1), :].bitcast(I32))
-        for gate, z in staged:
-            load_weights(gate, z, stage.tile([P, PACK, N], F32, name=f"raw_{gate}{z}", offset=place[gate, z]), nc.sync)
+        tables.append(load_words(1))
+        for n, (gate, z) in enumerate(late_passes):
+            load_pass(gate, z, stage.tile([P, PACK, N], F32, name=f"raw_{gate}{z}", offset=n * RAW_BYTES))
 
-        acc = {(gate, half): ps.tile([P, S], F32, name=f"acc_{gate}{half}")
+        acc = {(gate, half): [ps.tile([P, S], F32, name=f"acc_{gate}{half}")]
                for gate in "gif" for half in range(HALVES) if (gate, half) != ("f", 0)}
-        acc_first = [ps.tile([P, PIECE], F32, name=f"acc_f0{piece}") for piece in range(PIECES)]
+        acc["f", 0] = [ps.tile([P, PIECE], F32, name=f"acc_f0{piece}") for piece in range(PIECES)]
         x_codes = {}
         for z in range(PASSES):
             x_codes[z] = sb.tile([P, S], U32, name=f"x_codes{z}", align_bytes=64)
             nc.vector.tensor_copy(x_codes[z][:], tables[z][:].indirect(offsets[:]))
         cells = [load_cell(half) for half in range(HALVES)]
 
-        def multiply(sums, z, codes, scales, j0=0, j1=S):
-            nc.tensor.matmul_mx(out=sums, lhsT=codes.bitcast(FP8X4), lhsT_scale=scales,
-                                rhs=x_codes[z][:, j0:j1].bitcast(FP8X4), rhs_scale=x_sc[:, z * S + j0:z * S + j1],
-                                start=(z == 0), stop=(z == PASSES - 1))
+        def multiply(gate, half, z, codes, scales):
+            width = S // len(acc[gate, half])
+            for n, bank in enumerate(acc[gate, half]):
+                j0, j1 = n * width, (n + 1) * width
+                nc.tensor.matmul_mx(out=bank[:], lhsT=codes.bitcast(FP8X4), lhsT_scale=scales,
+                                    rhs=x_codes[z][:, j0:j1].bitcast(FP8X4), rhs_scale=x_sc[:, z * S + j0:z * S + j1],
+                                    start=(z == 0), stop=(z == PASSES - 1))
 
         def whole_pass(gate, z):
             codes, scales = quantize(interleave(nc.vector.tensor_copy, gate, z, 0, N), N, f"{gate}{z}")
             for half in range(HALVES):
                 cols = slice(half * P, (half + 1) * P)
-                multiply(acc[gate, half][:], z, codes[:, cols], scales[:, cols])
+                multiply(gate, half, z, codes[:, cols], scales[:, cols])
 
-        def cast_halves(gate, z, copies):
-            return [interleave(copy, gate, z, half * P, (half + 1) * P) for half, copy in enumerate(copies)]
+        def half_pass(gate, half, z, grouped, tag=None):
+            codes, scales = quantize(grouped, P, f"{gate}{z}{half}", tag)
+            multiply(gate, half, z, codes[:], scales[:])
 
-        def half_pass(gate, half, z, grouped, room=None):
-            codes, scales = quantize(grouped, P, f"{gate}{z}{half}", room)
-            if (gate, half) == ("f", 0):
-                for piece in range(PIECES):
-                    multiply(acc_first[piece][:], z, codes[:], scales[:], piece * PIECE, (piece + 1) * PIECE)
-            else:
-                multiply(acc[gate, half][:], z, codes[:], scales[:])
+        def pass_by_halves(gate, z):
+            grouped = [interleave(nc.vector.tensor_copy, gate, z, half * P, (half + 1) * P) for half in range(HALVES)]
+            for half in range(HALVES):
+                half_pass(gate, half, z, grouped[half])
 
         act = {}
 
-        def activate(gate, half, func, room):
-            act[gate, half] = room
-            nc.scalar.activation(out=room[:], in_=acc[gate, half][:], func=func)
+        def activate(gate, half, func):
+            act[gate, half] = sb.tile([P, S], F32, name=f"act_{gate}{half}", align_bytes=64)
+            width = S // len(acc[gate, half])
+            for n, bank in enumerate(acc[gate, half]):
+                nc.scalar.activation(out=act[gate, half][:, n * width:(n + 1) * width], in_=bank[:], func=func)
 
-        shared = (nc.vector.tensor_copy, nc.scalar.copy)
-        whole_pass("i", 0)
-        grouped = cast_halves("i", 1, (nc.vector.tensor_copy, nc.vector.tensor_copy))
+        for z in range(PASSES):
+            whole_pass("i", z)
         for half in range(HALVES):
-            half_pass("i", half, 1, grouped[half])
-        for half in range(HALVES):
-            activate("i", half, ACT.Sigmoid, sb.tile([P, S], F32, name=f"act_i{half}", align_bytes=64))
+            activate("i", half, ACT.Sigmoid)
         whole_pass("g", 0)
-        grouped = cast_halves("g", 1, (nc.vector.tensor_copy, nc.vector.tensor_copy))
+        pass_by_halves("g", 1)
+        pass_by_halves("f", 0)
         for half in range(HALVES):
-            half_pass("g", half, 1, grouped[half])
-        grouped = cast_halves("f", 0, shared)
-        for half in reversed(range(HALVES)):
-            half_pass("f", half, 0, grouped[half])
+            activate("g", half, ACT.Tanh)
+
+        first = interleave(nc.vector.tensor_copy, "f", 1, 0, P)
+        second = interleave(nc.scalar.copy, "f", 1, P, N, tag="codes_g11")
+        half_pass("f", 0, 1, first)
+        activate("f", 0, ACT.Sigmoid)
+        new = [raw["f", 1][:, :, :P], sb.tile([P, RUNS, P], F32, name="new1")[:]]
         for half in range(HALVES):
-            activate("g", half, ACT.Tanh, stage.tile([P, S], F32, name=f"act_g{half}",
-                                                     offset=place["f", 0] + half * ACT_BYTES, align_bytes=64))
-        grouped = cast_halves("f", 1, shared)
-        half_pass("f", 0, 1, grouped[0])
-        act["f", 0] = sb.tile([P, S], F32, name="act_f0", align_bytes=64)
-        for piece in range(PIECES):
-            nc.scalar.activation(out=act["f", 0][:, piece * PIECE:(piece + 1) * PIECE], in_=acc_first[piece][:], func=ACT.Sigmoid)
-        new = {}
-        for half in range(HALVES):
-            new[half] = raw["f", 1][:, :, :P] if half == 0 else sb.tile([P, PACK, P], F32, name="new1")[:]
             nc.vector.tensor_tensor(new[half], act["i", half][:].rearrange("p (run c) -> p run c", c=P),
                                     act["g", half][:].rearrange("p (run c) -> p run c", c=P), ALU.mult)
-        half_pass("f", 1, 1, grouped[1], stage.tile([P, P], U32, name="codes_f11", offset=place["f", 0], align_bytes=64))
-        activate("f", 1, ACT.Sigmoid, sb.tile([P, S], F32, name="act_f1", align_bytes=64))
+        half_pass("f", 1, 1, second, tag="act_g0")
+        activate("f", 1, ACT.Sigmoid)
 
-        runs = PIECE // P
+        runs = RUNS // PIECES
         for half in range(HALVES):
             kept = [sb.tile([P, PIECE], F32, name=f"kept{half}{piece}") for piece in range(PIECES)]
             for piece in range(PIECES):

@@ -164,16 +164,26 @@ def tile_picked_beamcell_none_p_kernel(tc, x_words, x_scales, w1, w2, w3, cell, 
         half_pass("f", 1, 1, second, tag="act_g0")
         activate("f", 1, ACT.Sigmoid)
 
-        runs = RUNS // PIECES
+        cuts = [(0, 2, 4), (0, 2, 3, 4)]
         for half in range(HALVES):
-            kept = [sb.tile([P, PIECE], F32, name=f"kept{half}{piece}") for piece in range(PIECES)]
-            for piece in range(PIECES):
-                entries = offsets[:, piece * PIECE // LIST_GROUP:(piece + 1) * PIECE // LIST_GROUP]
-                nc.vector.tensor_tensor(kept[piece][:], cells[half][:].indirect(entries),
-                                        act["f", half][:, piece * PIECE:(piece + 1) * PIECE], ALU.mult)
-            for piece in range(PIECES):
-                res = sb.tile([P, runs, P], F32, name=f"res{half}{piece}")
-                nc.vector.tensor_tensor(res[:], kept[piece][:].rearrange("p (run c) -> p run c", c=P),
-                                        new[half][:, runs * piece:runs * (piece + 1), :], ALU.add)
-                nc.sync.dma_start(out=out[half * P:(half + 1) * P, piece * PIECE:(piece + 1) * PIECE],
+            pieces = list(zip(cuts[half], cuts[half][1:]))
+            kept = {}
+
+            def gather(r0, r1):
+                kept[r0] = sb.tile([P, (r1 - r0) * P], F32, name=f"kept{half}{r0}")
+                entries = offsets[:, r0 * P // LIST_GROUP:r1 * P // LIST_GROUP]
+                nc.vector.tensor_tensor(kept[r0][:], cells[half][:].indirect(entries),
+                                        act["f", half][:, r0 * P:r1 * P], ALU.mult)
+
+            def finish(r0, r1, tag=None):
+                res = sb.tile([P, r1 - r0, P], F32, name=f"res{half}{r0}")
+                nc.vector.tensor_tensor(res[:], kept[r0][:].rearrange("p (run c) -> p run c", c=P),
+                                        new[half][:, r0:r1, :], ALU.add)
+                nc.sync.dma_start(out=out[half * P:(half + 1) * P, r0 * P:r1 * P],
                                   in_=res[:].rearrange("p run c -> p (run c)"))
+
+            gather(*pieces[0])
+            for n in range(1, len(pieces)):
+                gather(*pieces[n])
+                finish(*pieces[n - 1])
+            finish(*pieces[-1])

@@ -164,7 +164,7 @@ def tile_picked_beamcell_none_p_kernel(tc, x_words, x_scales, w1, w2, w3, cell, 
         half_pass("f", 1, 1, second, tag="act_g0")
         activate("f", 1, ACT.Sigmoid)
 
-        cuts = [(0, 2, 4), (0, 2, 3, 4)]
+        cuts = [(0, 2, 4), (0, 1, 3, 4)]
         for half in range(HALVES):
             pieces = list(zip(cuts[half], cuts[half][1:]))
             kept = {}

@@ -29,6 +29,7 @@ RAW_BYTES = PACK * N * 4
 ROW_BYTES = T * 4
 PIECES = 2
 PIECE = S // PIECES
+DMA_ALIGN = 256
 RUNS = S // P
 
 
@@ -47,7 +48,7 @@ def tile_picked_beamcell_none_p_kernel(tc, x_words, x_scales, w1, w2, w3, cell, 
         raw = {}
 
         def load_words(z):
-            table = stage.tile([P, T], U32, name=f"words{z}", offset=table_place[z])
+            table = stage.tile([P, T], U32, name=f"words{z}", offset=table_place[z], align_bytes=DMA_ALIGN)
             nc.sync.dma_start(out=table[:].bitcast(I32), in_=x_words[z].rearrange("p n t -> p (n t)").bitcast(I32))
             return table
 
@@ -57,7 +58,7 @@ def tile_picked_beamcell_none_p_kernel(tc, x_words, x_scales, w1, w2, w3, cell, 
             nc.sync.dma_start(out=room[:], in_=weights[gate][k_rows, :].rearrange("(p t) n -> p t n", t=PACK))
 
         def load_cell(half):
-            rows = stage.tile([P, T], F32, name=f"cell{half}", offset=table_place[half])
+            rows = stage.tile([P, T], F32, name=f"cell{half}", offset=table_place[half], align_bytes=DMA_ALIGN)
             nc.sync.dma_start(out=rows[:], in_=cell[half * P:(half + 1) * P, :])
             return rows
 
@@ -75,24 +76,24 @@ def tile_picked_beamcell_none_p_kernel(tc, x_words, x_scales, w1, w2, w3, cell, 
                                   in_=grouped[:].rearrange("p c t -> p (c t)"))
             return codes, scales
 
-        scale_table = stage.tile([P, held_bytes], U8, name="scale_table", offset=0)
+        scale_table = stage.tile([P, held_bytes], U8, name="scale_table", offset=0, align_bytes=DMA_ALIGN)
         nc.sync.dma_start(out=scale_table[0:SCALE_ROWS, :T].bitcast(I32),
                           in_=x_scales.bitcast(I32).rearrange("z r c -> r z c"))
         offsets = sb.tile([P, S // LIST_GROUP], U16, name="offsets")
         nc.sync.dma_start(offsets[:], offs)
         tables = [load_words(0)]
-        raw_i = sb.tile([P, PASSES, PACK, N], F32, name="raw_i")
+        raw_i = sb.tile([P, PASSES, PACK, N], F32, name="raw_i", align_bytes=DMA_ALIGN)
         nc.sync.dma_start(out=raw_i[:].rearrange("p z t n -> p z (t n)"),
                           in_=weights["i"].rearrange("(z p t) n -> p z (t n)", p=P, t=PACK))
         for z in range(PASSES):
             raw["i", z] = raw_i[:, z]
-        load_pass("g", 0, sb.tile([P, PACK, N], F32, name="raw_g0"))
+        load_pass("g", 0, sb.tile([P, PACK, N], F32, name="raw_g0", align_bytes=DMA_ALIGN))
         nc.vector.memset(scale_table[2 * QUADRANT:P, :T].bitcast(I32), 0)
         nc.vector.memset(scale_table[QUADRANT:2 * QUADRANT, :T].bitcast(I32), 0)
 
-        x_sc = sb.tile([P, PASSES * S], U8, name="x_sc", align_bytes=64)
+        x_sc = sb.tile([P, PASSES * S], U8, name="x_sc", align_bytes=DMA_ALIGN)
         nc.vector.memset(x_sc[:].bitcast(I32), 0)
-        picked_sc = sb.tile([P, S], U8, name="picked_sc")
+        picked_sc = sb.tile([P, S], U8, name="picked_sc", align_bytes=DMA_ALIGN)
         nc.vector.tensor_copy(picked_sc[:], scale_table[:, :T].indirect(offsets[:]))
         picked_rows = ROWS_IN_QUADRANT * PASSES
         for q in (0, 2, 1, 3):
@@ -101,7 +102,7 @@ def tile_picked_beamcell_none_p_kernel(tc, x_words, x_scales, w1, w2, w3, cell, 
                 in_=picked_sc[picked_rows * q:picked_rows * (q + 1), :].bitcast(I32))
         tables.append(load_words(1))
         for n, (gate, z) in enumerate(late_passes):
-            load_pass(gate, z, stage.tile([P, PACK, N], F32, name=f"raw_{gate}{z}", offset=n * RAW_BYTES))
+            load_pass(gate, z, stage.tile([P, PACK, N], F32, name=f"raw_{gate}{z}", offset=n * RAW_BYTES, align_bytes=DMA_ALIGN))
 
         acc = {(gate, half): [ps.tile([P, S], F32, name=f"acc_{gate}{half}")]
                for gate in "gif" for half in range(HALVES) if (gate, half) != ("f", 0)}
@@ -176,7 +177,7 @@ def tile_picked_beamcell_none_p_kernel(tc, x_words, x_scales, w1, w2, w3, cell, 
                                         act["f", half][:, r0 * P:r1 * P], ALU.mult)
 
             def finish(r0, r1, tag=None):
-                res = sb.tile([P, r1 - r0, P], F32, name=f"res{half}{r0}")
+                res = sb.tile([P, r1 - r0, P], F32, name=f"res{half}{r0}", align_bytes=DMA_ALIGN)
                 nc.vector.tensor_tensor(res[:], kept[r0][:].rearrange("p (run c) -> p run c", c=P),
                                         new[half][:, r0:r1, :], ALU.add)
                 nc.sync.dma_start(out=out[half * P:(half + 1) * P, r0 * P:r1 * P],

@@ -29,8 +29,10 @@ RAW_BYTES = PACK * N * 4
 ROW_BYTES = T * 4
 PIECES = 2
 PIECE = S // PIECES
-DMA_ALIGN = 256
 RUNS = S // P
+MX_ALIGN = 64
+DMA_ALIGN = 256
+CUTS = ((0, 2, 4), (0, 2, 3, 4))
 
 
 def tile_picked_beamcell_none_p_kernel(tc, x_words, x_scales, w1, w2, w3, cell, offs, out):
@@ -64,14 +66,14 @@ def tile_picked_beamcell_none_p_kernel(tc, x_words, x_scales, w1, w2, w3, cell, 
 
         def interleave(copy, gate, z, c0, c1, tag=None):
             name = f"bf_{gate}{z}_{c0}"
-            grouped = sb.tile([P, c1 - c0, PACK], BF16, name=name, tag=tag or name, align_bytes=64)
+            grouped = sb.tile([P, c1 - c0, PACK], BF16, name=name, tag=tag or name, align_bytes=MX_ALIGN)
             copy(out=grouped[:].rearrange("p (c i) t -> p c t i", i=LINE),
                  in_=raw[gate, z][:, :, c0:c1].rearrange("p t (c i) -> p c t i", i=LINE))
             return grouped
 
         def quantize(grouped, width, name, tag=None):
-            codes = sb.tile([P, width], U32, name=f"codes_{name}", tag=tag or f"codes_{name}", align_bytes=64)
-            scales = sb.tile([P, width], U8, name=f"scales_{name}", align_bytes=64)
+            codes = sb.tile([P, width], U32, name=f"codes_{name}", tag=tag or f"codes_{name}", align_bytes=MX_ALIGN)
+            scales = sb.tile([P, width], U8, name=f"scales_{name}", align_bytes=MX_ALIGN)
             nc.vector.quantize_mx(out=codes[:].bitcast(FP8X4), scales=scales[:],
                                   in_=grouped[:].rearrange("p c t -> p (c t)"))
             return codes, scales
@@ -109,7 +111,7 @@ def tile_picked_beamcell_none_p_kernel(tc, x_words, x_scales, w1, w2, w3, cell, 
         acc["f", 0] = [ps.tile([P, PIECE], F32, name=f"acc_f0{piece}") for piece in range(PIECES)]
         x_codes = {}
         for z in range(PASSES):
-            x_codes[z] = sb.tile([P, S], U32, name=f"x_codes{z}", align_bytes=64)
+            x_codes[z] = sb.tile([P, S], U32, name=f"x_codes{z}", align_bytes=MX_ALIGN)
             nc.vector.tensor_copy(x_codes[z][:], tables[z][:].indirect(offsets[:]))
         cells = [load_cell(half) for half in range(HALVES)]
 
@@ -139,7 +141,7 @@ def tile_picked_beamcell_none_p_kernel(tc, x_words, x_scales, w1, w2, w3, cell, 
         act = {}
 
         def activate(gate, half, func):
-            act[gate, half] = sb.tile([P, S], F32, name=f"act_{gate}{half}", align_bytes=64)
+            act[gate, half] = sb.tile([P, S], F32, name=f"act_{gate}{half}", align_bytes=MX_ALIGN)
             width = S // len(acc[gate, half])
             for n, bank in enumerate(acc[gate, half]):
                 nc.scalar.activation(out=act[gate, half][:, n * width:(n + 1) * width], in_=bank[:], func=func)
@@ -165,26 +167,26 @@ def tile_picked_beamcell_none_p_kernel(tc, x_words, x_scales, w1, w2, w3, cell, 
         half_pass("f", 1, 1, second, tag="act_g0")
         activate("f", 1, ACT.Sigmoid)
 
-        cuts = [(0, 2, 4), (0, 1, 3, 4)]
+        def gather(half, r0, r1):
+            if r0 == RUNS - 1:
+                kept = act["f", half][:, :P]
+            else:
+                kept = sb.tile([P, (r1 - r0) * P], F32, name=f"kept{half}{r0}")[:]
+            entries = offsets[:, r0 * P // LIST_GROUP:r1 * P // LIST_GROUP]
+            nc.vector.tensor_tensor(kept, cells[half][:].indirect(entries), act["f", half][:, r0 * P:r1 * P], ALU.mult)
+            return kept
+
+        def finish(half, r0, r1, kept):
+            res = sb.tile([P, r1 - r0, P], F32, name=f"res{half}{r0}", align_bytes=DMA_ALIGN)
+            nc.vector.tensor_tensor(res[:], kept.rearrange("p (run c) -> p run c", c=P), new[half][:, r0:r1, :], ALU.add)
+            nc.sync.dma_start(out=out[half * P:(half + 1) * P, r0 * P:r1 * P],
+                              in_=res[:].rearrange("p run c -> p (run c)"))
+
         for half in range(HALVES):
-            pieces = list(zip(cuts[half], cuts[half][1:]))
-            kept = {}
-
-            def gather(r0, r1):
-                kept[r0] = sb.tile([P, (r1 - r0) * P], F32, name=f"kept{half}{r0}")
-                entries = offsets[:, r0 * P // LIST_GROUP:r1 * P // LIST_GROUP]
-                nc.vector.tensor_tensor(kept[r0][:], cells[half][:].indirect(entries),
-                                        act["f", half][:, r0 * P:r1 * P], ALU.mult)
-
-            def finish(r0, r1, tag=None):
-                res = sb.tile([P, r1 - r0, P], F32, name=f"res{half}{r0}", align_bytes=DMA_ALIGN)
-                nc.vector.tensor_tensor(res[:], kept[r0][:].rearrange("p (run c) -> p run c", c=P),
-                                        new[half][:, r0:r1, :], ALU.add)
-                nc.sync.dma_start(out=out[half * P:(half + 1) * P, r0 * P:r1 * P],
-                                  in_=res[:].rearrange("p run c -> p (run c)"))
-
-            gather(*pieces[0])
-            for n in range(1, len(pieces)):
-                gather(*pieces[n])
-                finish(*pieces[n - 1])
-            finish(*pieces[-1])
+            pieces = list(zip(CUTS[half], CUTS[half][1:]))
+            waiting = gather(half, *pieces[0])
+            for before, piece in zip(pieces, pieces[1:]):
+                gathered = gather(half, *piece)
+                finish(half, *before, waiting)
+                waiting = gathered
+            finish(half, *pieces[-1], waiting)

@@ -32,7 +32,6 @@ PIECE = S // PIECES
 RUNS = S // P
 MX_ALIGN = 64
 DMA_ALIGN = 256
-CUTS = ((0, 2, 4), (0, 2, 3, 4))
 
 
 def tile_picked_beamcell_none_p_kernel(tc, x_words, x_scales, w1, w2, w3, cell, offs, out):
@@ -167,26 +166,36 @@ def tile_picked_beamcell_none_p_kernel(tc, x_words, x_scales, w1, w2, w3, cell, 
         half_pass("f", 1, 1, second, tag="act_g0")
         activate("f", 1, ACT.Sigmoid)
 
-        def gather(half, r0, r1):
-            if r0 == RUNS - 1:
-                kept = act["f", half][:, :P]
-            else:
-                kept = sb.tile([P, (r1 - r0) * P], F32, name=f"kept{half}{r0}")[:]
-            entries = offsets[:, r0 * P // LIST_GROUP:r1 * P // LIST_GROUP]
-            nc.vector.tensor_tensor(kept, cells[half][:].indirect(entries), act["f", half][:, r0 * P:r1 * P], ALU.mult)
+        def entries(r0, r1):
+            return offsets[:, r0 * P // LIST_GROUP:r1 * P // LIST_GROUP]
+
+        def product(half, r0, r1, value):
+            kept = sb.tile([P, (r1 - r0) * P], F32, name=f"kept{half}{r0}")
+            nc.vector.tensor_tensor(kept[:], value, act["f", half][:, r0 * P:r1 * P], ALU.mult)
             return kept
 
-        def finish(half, r0, r1, kept):
-            res = sb.tile([P, r1 - r0, P], F32, name=f"res{half}{r0}", align_bytes=DMA_ALIGN)
-            nc.vector.tensor_tensor(res[:], kept.rearrange("p (run c) -> p run c", c=P), new[half][:, r0:r1, :], ALU.add)
-            nc.sync.dma_start(out=out[half * P:(half + 1) * P, r0 * P:r1 * P],
-                              in_=res[:].rearrange("p run c -> p (run c)"))
+        def total(half, r0, r1, kept, res):
+            nc.vector.tensor_tensor(res[:, r0:r1, :], kept[:].rearrange("p (run c) -> p run c", c=P), new[half][:, r0:r1, :], ALU.add)
 
-        for half in range(HALVES):
-            pieces = list(zip(CUTS[half], CUTS[half][1:]))
-            waiting = gather(half, *pieces[0])
-            for before, piece in zip(pieces, pieces[1:]):
-                gathered = gather(half, *piece)
-                finish(half, *before, waiting)
-                waiting = gathered
-            finish(half, *pieces[-1], waiting)
+        def store(half, r0, r1, res):
+            nc.sync.dma_start(out=out[half * P:(half + 1) * P, r0 * P:r1 * P],
+                              in_=res[:, r0:r1, :].rearrange("p run c -> p (run c)"))
+
+        res = [sb.tile([P, RUNS, P], F32, name=f"res{half}", align_bytes=DMA_ALIGN) for half in range(HALVES)]
+        kept = [product(0, r0, r0 + 2, cells[0][:].indirect(entries(r0, r0 + 2))) for r0 in (0, 2)]
+        for n, r0 in enumerate((0, 2)):
+            total(0, r0, r0 + 2, kept[n], res[0])
+            store(0, r0, r0 + 2, res[0])
+
+        picked = sb.tile([P, 2, P], F32, name="picked", tag="act_g0", align_bytes=MX_ALIGN)
+        for n in range(2):
+            nc.scalar.activation(out=picked[:, n, :], in_=cells[1][:].indirect(entries(2 + n, 3 + n)), func=ACT.Copy)
+        kept = [product(1, run, run + 1, cells[1][:].indirect(entries(run, run + 1))) for run in range(2)]
+        total(1, 0, 1, kept[0], res[1])
+        store(1, 0, 1, res[1])
+        kept.extend([product(1, 2 + n, 3 + n, picked[:, n, :]) for n in range(2)])
+        total(1, 1, 2, kept[1], res[1])
+        store(1, 1, 2, res[1])
+        total(1, 2, 3, kept[2], res[1])
+        total(1, 3, 4, kept[3], res[1])
+        store(1, 2, 4, res[1])

from contextlib import ExitStack

import concourse.mybir as mybir

K, T, S, N = 1024, 2048, 512, 256
FLOPS = 3 * 2 * K * N * S

F32 = mybir.dt.float32
BF16 = mybir.dt.bfloat16
I32 = mybir.dt.int32
U32 = mybir.dt.uint32
U16 = mybir.dt.uint16
U8 = mybir.dt.uint8
FP8X4 = mybir.dt.float8_e4m3fn_x4
ACT = mybir.ActivationFunctionType
ALU = mybir.AluOpType

P = 128
PACK = 4
K_PASS = P * PACK
PASSES = K // K_PASS
HALVES = N // P
QUADRANT = 32
SCALE_ROWS = K // 32
ROWS_IN_QUADRANT = 4
LIST_GROUP = 16
LINE = 4
RAW_BYTES = PACK * N * 4
ROW_BYTES = T * 4
PIECES = 2
PIECE = S // PIECES
RUNS = S // P
MX_ALIGN = 64
DMA_ALIGN = 256


def tile_picked_beamcell_none_p_kernel(tc, x_words, x_scales, w1, w2, w3, cell, offs, out):
    nc = tc.nc
    with ExitStack() as ctx:
        sb = ctx.enter_context(tc.tile_pool(name="sb", bufs=1))
        stage = ctx.enter_context(tc.tile_pool(name="stage", bufs=1))
        ps = ctx.enter_context(tc.psum_pool(name="ps", bufs=1))

        weights = {"i": w2, "g": w3, "f": w1}
        late_passes = (("g", 1), ("f", 0), ("f", 1))
        late_bytes = len(late_passes) * RAW_BYTES
        held_bytes = late_bytes + ROW_BYTES
        table_place = (held_bytes, late_bytes)
        raw = {}

        def load_words(z):
            table = stage.tile([P, T], U32, name=f"words{z}", offset=table_place[z], align_bytes=DMA_ALIGN)
            nc.sync.dma_start(out=table[:].bitcast(I32), in_=x_words[z].rearrange("p n t -> p (n t)").bitcast(I32))
            return table

        def load_pass(gate, z, room):
            raw[gate, z] = room
            k_rows = slice(z * K_PASS, (z + 1) * K_PASS)
            nc.sync.dma_start(out=room[:], in_=weights[gate][k_rows, :].rearrange("(p t) n -> p t n", t=PACK))

        def load_cell(half):
            rows = stage.tile([P, T], F32, name=f"cell{half}", offset=table_place[half], align_bytes=DMA_ALIGN)
            nc.sync.dma_start(out=rows[:], in_=cell[half * P:(half + 1) * P, :])
            return rows

        def interleave(copy, gate, z, c0, c1, tag=None):
            name = f"bf_{gate}{z}_{c0}"
            grouped = sb.tile([P, c1 - c0, PACK], BF16, name=name, tag=tag or name, align_bytes=MX_ALIGN)
            copy(out=grouped[:].rearrange("p (c i) t -> p c t i", i=LINE),
                 in_=raw[gate, z][:, :, c0:c1].rearrange("p t (c i) -> p c t i", i=LINE))
            return grouped

        def quantize(grouped, width, name, tag=None):
            codes = sb.tile([P, width], U32, name=f"codes_{name}", tag=tag or f"codes_{name}", align_bytes=MX_ALIGN)
            scales = sb.tile([P, width], U8, name=f"scales_{name}", align_bytes=MX_ALIGN)
            nc.vector.quantize_mx(out=codes[:].bitcast(FP8X4), scales=scales[:],
                                  in_=grouped[:].rearrange("p c t -> p (c t)"))
            return codes, scales

        scale_table = stage.tile([P, held_bytes], U8, name="scale_table", offset=0, align_bytes=DMA_ALIGN)
        nc.sync.dma_start(out=scale_table[0:SCALE_ROWS, :T].bitcast(I32),
                          in_=x_scales.bitcast(I32).rearrange("z r c -> r z c"))
        offsets = sb.tile([P, S // LIST_GROUP], U16, name="offsets")
        nc.sync.dma_start(offsets[:], offs)
        tables = [load_words(0)]
        raw_i = sb.tile([P, PASSES, PACK, N], F32, name="raw_i", align_bytes=DMA_ALIGN)
        nc.sync.dma_start(out=raw_i[:].rearrange("p z t n -> p z (t n)"),
                          in_=weights["i"].rearrange("(z p t) n -> p z (t n)", p=P, t=PACK))
        for z in range(PASSES):
            raw["i", z] = raw_i[:, z]
        load_pass("g", 0, sb.tile([P, PACK, N], F32, name="raw_g0", align_bytes=DMA_ALIGN))
        nc.vector.memset(scale_table[2 * QUADRANT:P, :T].bitcast(I32), 0)
        nc.vector.memset(scale_table[QUADRANT:2 * QUADRANT, :T].bitcast(I32), 0)

        x_sc = sb.tile([P, PASSES * S], U8, name="x_sc", align_bytes=DMA_ALIGN)
        nc.vector.memset(x_sc[:].bitcast(I32), 0)
        picked_sc = sb.tile([P, S], U8, name="picked_sc", align_bytes=DMA_ALIGN)
        nc.vector.tensor_copy(picked_sc[:], scale_table[:, :T].indirect(offsets[:]))
        picked_rows = ROWS_IN_QUADRANT * PASSES
        for q in (0, 2, 1, 3):
            nc.sync.dma_start(
                out=x_sc[QUADRANT * q:QUADRANT * q + ROWS_IN_QUADRANT, :].bitcast(I32).rearrange("s (z c) -> s z c", z=PASSES),
                in_=picked_sc[picked_rows * q:picked_rows * (q + 1), :].bitcast(I32))
        tables.append(load_words(1))
        for n, (gate, z) in enumerate(late_passes):
            load_pass(gate, z, stage.tile([P, PACK, N], F32, name=f"raw_{gate}{z}", offset=n * RAW_BYTES, align_bytes=DMA_ALIGN))

        acc = {(gate, half): [ps.tile([P, S], F32, name=f"acc_{gate}{half}")]
               for gate in "gif" for half in range(HALVES) if (gate, half) != ("f", 0)}
        acc["f", 0] = [ps.tile([P, PIECE], F32, name=f"acc_f0{piece}") for piece in range(PIECES)]
        x_codes = {}
        for z in range(PASSES):
            x_codes[z] = sb.tile([P, S], U32, name=f"x_codes{z}", align_bytes=MX_ALIGN)
            nc.vector.tensor_copy(x_codes[z][:], tables[z][:].indirect(offsets[:]))
        cells = [load_cell(half) for half in range(HALVES)]

        def multiply(gate, half, z, codes, scales):
            width = S // len(acc[gate, half])
            for n, bank in enumerate(acc[gate, half]):
                j0, j1 = n * width, (n + 1) * width
                nc.tensor.matmul_mx(out=bank[:], lhsT=codes.bitcast(FP8X4), lhsT_scale=scales,
                                    rhs=x_codes[z][:, j0:j1].bitcast(FP8X4), rhs_scale=x_sc[:, z * S + j0:z * S + j1],
                                    start=(z == 0), stop=(z == PASSES - 1))

        def whole_pass(gate, z):
            codes, scales = quantize(interleave(nc.vector.tensor_copy, gate, z, 0, N), N, f"{gate}{z}")
            for half in range(HALVES):
                cols = slice(half * P, (half + 1) * P)
                multiply(gate, half, z, codes[:, cols], scales[:, cols])

        def half_pass(gate, half, z, grouped, tag=None):
            codes, scales = quantize(grouped, P, f"{gate}{z}{half}", tag)
            multiply(gate, half, z, codes[:], scales[:])

        def pass_by_halves(gate, z):
            grouped = [interleave(nc.vector.tensor_copy, gate, z, half * P, (half + 1) * P) for half in range(HALVES)]
            for half in range(HALVES):
                half_pass(gate, half, z, grouped[half])

        act = {}

        def activate(gate, half, func):
            act[gate, half] = sb.tile([P, S], F32, name=f"act_{gate}{half}", align_bytes=MX_ALIGN)
            width = S // len(acc[gate, half])
            for n, bank in enumerate(acc[gate, half]):
                nc.scalar.activation(out=act[gate, half][:, n * width:(n + 1) * width], in_=bank[:], func=func)

        for z in range(PASSES):
            whole_pass("i", z)
        for half in range(HALVES):
            activate("i", half, ACT.Sigmoid)
        whole_pass("g", 0)
        pass_by_halves("g", 1)
        pass_by_halves("f", 0)
        for half in range(HALVES):
            activate("g", half, ACT.Tanh)

        first = interleave(nc.vector.tensor_copy, "f", 1, 0, P)
        second = interleave(nc.scalar.copy, "f", 1, P, N, tag="codes_g11")
        half_pass("f", 0, 1, first)
        activate("f", 0, ACT.Sigmoid)
        new = [raw["f", 1][:, :, :P], sb.tile([P, RUNS, P], F32, name="new1")[:]]
        for half in range(HALVES):
            nc.vector.tensor_tensor(new[half], act["i", half][:].rearrange("p (run c) -> p run c", c=P),
                                    act["g", half][:].rearrange("p (run c) -> p run c", c=P), ALU.mult)
        half_pass("f", 1, 1, second, tag="act_g0")
        activate("f", 1, ACT.Sigmoid)

        def entries(r0, r1):
            return offsets[:, r0 * P // LIST_GROUP:r1 * P // LIST_GROUP]

        def product(half, r0, r1, value):
            kept = sb.tile([P, (r1 - r0) * P], F32, name=f"kept{half}{r0}")
            nc.vector.tensor_tensor(kept[:], value, act["f", half][:, r0 * P:r1 * P], ALU.mult)
            return kept

        def total(half, r0, r1, kept, res):
            nc.vector.tensor_tensor(res[:, r0:r1, :], kept[:].rearrange("p (run c) -> p run c", c=P), new[half][:, r0:r1, :], ALU.add)

        def store(half, r0, r1, res):
            nc.sync.dma_start(out=out[half * P:(half + 1) * P, r0 * P:r1 * P],
                              in_=res[:, r0:r1, :].rearrange("p run c -> p (run c)"))

        res = [sb.tile([P, RUNS, P], F32, name=f"res{half}", align_bytes=DMA_ALIGN) for half in range(HALVES)]
        kept = [product(0, r0, r0 + 2, cells[0][:].indirect(entries(r0, r0 + 2))) for r0 in (0, 2)]
        for n, r0 in enumerate((0, 2)):
            total(0, r0, r0 + 2, kept[n], res[0])
            store(0, r0, r0 + 2, res[0])

        picked = sb.tile([P, 2, P], F32, name="picked", tag="act_g0", align_bytes=MX_ALIGN)
        for n in range(2):
            nc.scalar.activation(out=picked[:, n, :], in_=cells[1][:].indirect(entries(2 + n, 3 + n)), func=ACT.Copy)
        kept = [product(1, run, run + 1, cells[1][:].indirect(entries(run, run + 1))) for run in range(2)]
        total(1, 0, 1, kept[0], res[1])
        store(1, 0, 1, res[1])
        kept.extend([product(1, 2 + n, 3 + n, picked[:, n, :]) for n in range(2)])
        total(1, 1, 2, kept[1], res[1])
        store(1, 1, 2, res[1])
        total(1, 2, 3, kept[2], res[1])
        total(1, 3, 4, kept[3], res[1])
        store(1, 2, 4, res[1])
